import numpy as np
import ml_dtypes


def mxq(x, axis, fmt="e4m3"):
    dtype, down = {"e4m3": (ml_dtypes.float8_e4m3fn, 7), "e5m2": (ml_dtypes.float8_e5m2, 14)}[fmt]
    v = np.moveaxis(np.asarray(x, np.float32).astype(ml_dtypes.bfloat16).astype(np.float64), axis, -1)
    blocks = v.reshape(v.shape[:-1] + (-1, 32))
    amax = np.abs(blocks).max(-1, keepdims=True)
    byte = np.maximum(np.where(amax > 0, np.frexp(amax)[1] - 1 + 127, 0) - down, 1)
    scale = np.exp2(byte - 127.0)
    codes = (blocks / scale).astype(np.float32).astype(dtype).astype(np.float64)
    return np.moveaxis((codes * scale).reshape(v.shape), -1, axis)


WIDE = False


def mx_kscale(k):
    if not WIDE:
        return np.ones(k)
    levels = np.array([18, -18])
    if k % 512:
        return np.exp2(np.random.permutation(np.resize(levels, k // 32))).repeat(32)
    a = np.empty((k // 512, 16))
    for p in range(k // 512):
        a[p, :8] = np.random.permutation(np.resize(levels, 8))
        for g in range(8):
            far = levels[np.abs(levels - a[p, g]) >= 10]
            a[p, g + 8] = far[np.random.randint(len(far))]
    return np.exp2(a.ravel()).repeat(32)


def f64(x):
    return np.asarray(x).astype(np.float64)


def striped(idx):
    return np.tile(np.asarray(idx).reshape(-1, 16).T, (8, 1)).astype(np.uint16)


def unstriped(offs):
    return offs[:16].T.reshape(-1).astype(np.int64)

def planes(y):
    n, m = y.shape
    v = y.astype(np.float32).astype(ml_dtypes.bfloat16).astype(np.float64).reshape(n // 32, 32, m)
    top = np.abs(v).max(1)
    byte = np.clip(np.where(top > 0, np.frexp(top)[1] - 1 + 127 - 7, 1), 1, 254)
    codes = (v * np.exp2(127.0 - byte)[:, None, :]).reshape(n, m).astype(np.float32).astype(ml_dtypes.float8_e4m3fn).view(np.uint8)
    words = codes.reshape(n // 512, 128, 4, m).transpose(0, 1, 3, 2)
    return np.ascontiguousarray(words), np.ascontiguousarray(byte.astype(np.uint8).reshape(n // 512, 16, m))


def setup_inputs():
    n = np.random.standard_normal
    uni = np.random.uniform
    ia = np.random.permutation(2048)[:512]
    ib = np.random.randint(0, 1024, 512)
    ic = np.random.randint(0, 1024, 512)
    f_f = mx_kscale(512)
    return {
        "bT": (np.round(n((512, 1024)) * 4) / 4).astype(np.float32),
        "cT": (np.round(n((512, 1024)) * 4) / 4 * f_f[:, None]).astype(np.float32),
        "er": np.tile(np.random.randint(-16, 17, 512) / 8.0, (128, 1)).astype(np.float32),
        "C": (n((512, 512)) / np.sqrt(512) / f_f[:, None]).astype(np.float32),
        "aoffs": striped(ia),
        "boffs": striped(ib),
        "coffs": striped(ic),
    }


def reference(bT, cT, er, C, aoffs, boffs, coffs):
    ia = unstriped(aoffs)
    ib = unstriped(boffs)
    ic = unstriped(coffs)
    b = f64(bT)[:, ib]
    c = f64(cT)[:, ic]
    q = f64(er)[:1] * b * c
    da = mxq(f64(C), 0, "e4m3").T @ mxq(q, 0, "e5m2")
    out_0 = np.zeros((512, 2048))
    out_0[:, ia] = da
    return (out_0,) + planes(out_0)

@@ -1,0 +1,160 @@
+from contextlib import ExitStack
+
+import concourse.mybir as mybir
+
+F32 = mybir.dt.float32
+BF16 = mybir.dt.bfloat16
+I32 = mybir.dt.int32
+U32 = mybir.dt.uint32
+U16 = mybir.dt.uint16
+U8 = mybir.dt.uint8
+E4M3 = mybir.dt.float8_e4m3fn_x4
+E5M2 = mybir.dt.float8_e5m2_x4
+MULT = mybir.AluOpType.mult
+
+P = 128
+LANES = 4
+F = 512
+D = 512
+N = 512
+T = 2048
+U = 1024
+WIDTHS = (256, 256, 512, 512, 256, 256)
+
+FLOPS = 2 * F * D * N
+
+
+def tile_attend_gtucker_pl_kernel(tc, bT, cT, er, C, aoffs, boffs, coffs, out_0, out_1, out_2):
+    nc = tc.nc
+    with ExitStack() as ctx:
+        lists = ctx.enter_context(tc.tile_pool(name="lists", bufs=1))
+        sb = ctx.enter_context(tc.tile_pool(name="sb", bufs=1))
+        psum = ctx.enter_context(tc.psum_pool(name="psum", bufs=1))
+
+        a_list = lists.tile([P, N // 16], U16, name="a_list")
+        b_list = lists.tile([P, N // 16], U16, name="b_list")
+        c_list = lists.tile([P, N // 16], U16, name="c_list")
+
+        b_rows = bT.rearrange("(p t) u -> p t u", t=LANES)
+        c_rows = cT.rearrange("(p t) u -> p t u", t=LANES)
+        core_rows = C.rearrange("(p j) d -> p j d", j=LANES)
+        out_rows = out_0.rearrange("(p t) c -> p t c", t=LANES)
+        out_words = out_1[0].rearrange("p c l -> p (c l)").bitcast(I32)
+        out_scales = out_2[0].bitcast(I32)
+
+        b_tab = [sb.tile([P, U], F32, name="b_tab%d" % t) for t in range(LANES)]
+        c_tab = [sb.tile([P, U], F32, name="c_tab%d" % t) for t in range(LANES)]
+        er_sb = sb.tile([P, N], F32, name="er_sb")
+        half = D // 2
+        core = [sb.tile([P, LANES, half], F32, name="core%d" % h) for h in range(2)]
+
+        nc.sync.dma_start(b_list[:], boffs)
+        nc.sync.dma_start(b_tab[0][:], b_rows[:, 0, :])
+        nc.sync.dma_start(er_sb[:], er)
+        nc.sync.dma_start(c_list[:], coffs)
+        nc.sync.dma_start(c_tab[0][:], c_rows[:, 0, :])
+        for t in range(1, LANES):
+            if t >= 2:
+                h = t - 2
+                nc.sync.dma_start(core[h][:], core_rows[:, :, h * half:(h + 1) * half])
+            nc.sync.dma_start(b_tab[t][:], b_rows[:, t, :])
+            nc.sync.dma_start(c_tab[t][:], c_rows[:, t, :])
+        nc.sync.dma_start(a_list[:], aoffs)
+
+        window = [None] * LANES
+        for t in range(3):
+            window[t] = sb.tile([P, T], F32, name="window%d" % t)
+            nc.vector.memset(window[t][:].bitcast(I32), 0)
+
+        q_bf = sb.tile([P, N, LANES], BF16, name="q_bf", tag="q_bf", align_bytes=64)
+        q_pair = [sb.tile([P, 2, N], F32, name="q_pair%d" % h) for h in range(2)]
+        eb = [sb.tile([P, N], F32, name="eb%d" % h) for h in range(2)]
+        for t in range(LANES):
+            h, e = divmod(t, 2)
+            nc.vector.tensor_tensor(eb[e][:], b_tab[t][:].indirect(b_list[:]), er_sb[:], MULT)
+            nc.vector.tensor_tensor(q_pair[h][:, e, :], c_tab[t][:].indirect(c_list[:]), eb[e][:], MULT)
+            if t == 1:
+                nc.scalar.copy(q_bf[:, :, 0:2], q_pair[0][:].rearrange("p e i -> p i e"))
+        nc.vector.tensor_copy(q_bf[:, :, 2:4], q_pair[1][:].rearrange("p e i -> p i e"))
+
+        core_bf = sb.tile([P, LANES, P, LANES], BF16, name="core_bf", align_bytes=64)
+        mh = P // 2
+        for h in range(2):
+            nc.scalar.copy(
+                core_bf[:, :, h * mh:(h + 1) * mh, :].rearrange("p t m j -> p m j t"),
+                core[h][:].rearrange("p j (m t) -> p m j t", t=LANES),
+            )
+        core_codes = sb.tile([P, LANES, P], U32, name="core_codes", align_bytes=64)
+        core_scales = sb.tile([P, LANES, P], U8, name="core_scales", align_bytes=64)
+        q_codes = sb.tile([P, N], U32, name="q_codes", align_bytes=64)
+        q_scales = sb.tile([P, N], U8, name="q_scales", align_bytes=64)
+
+        def quantise_core(t):
+            nc.vector.quantize_mx(
+                out=core_codes[:, t, :].bitcast(E4M3),
+                scales=core_scales[:, t, :],
+                in_=core_bf[:, t, :, :].rearrange("p m j -> p (m j)"),
+            )
+
+        quantise_core(0)
+        nc.vector.quantize_mx(out=q_codes[:].bitcast(E5M2), scales=q_scales[:], in_=q_bf[:].rearrange("p i t -> p (i t)"))
+        for t in range(1, LANES):
+            quantise_core(t)
+        window[3] = sb.tile([P, T], F32, name="window3", tag="q_bf", align_bytes=64)
+        nc.vector.memset(window[3][:].bitcast(I32), 0)
+
+        da = []
+        for t in range(LANES):
+            acc = psum.tile([P, N], F32, name="acc%d" % t)
+            nc.tensor.matmul_mx(
+                out=acc[:],
+                lhsT=core_codes[:, t, :].bitcast(E4M3),
+                lhsT_scale=core_scales[:, t, :],
+                rhs=q_codes[:].bitcast(E5M2),
+                rhs_scale=q_scales[:],
+                start=True,
+                stop=True,
+            )
+            da_t = sb.tile([P, N], F32, name="da%d" % t)
+            nc.scalar.copy(da_t[:], acc[:])
+            da.append(da_t)
+
+        chunks = len(WIDTHS)
+        cols = [slice(sum(WIDTHS[:j]), sum(WIDTHS[:j + 1])) for j in range(chunks)]
+        pairs = [sb.tile([P, 2, WIDTHS[j], 2], BF16, name="pairs%d" % j, align_bytes=64) for j in range(chunks)]
+        for t in range(LANES):
+            h, e = divmod(t, 2)
+            nc.vector.tensor_copy(window[t][:].indirect(a_list[:]), da[t][:])
+            nc.sync.dma_start(out_rows[:, t, :], window[t][:])
+            for j in range(chunks):
+                nc.scalar.copy(pairs[j][:, h, :, e], window[t][:, cols[j]])
+
+        y_scales = sb.tile([P, T], U8, name="y_scales", align_bytes=64)
+        y_bf = [sb.tile([P, WIDTHS[j], LANES], BF16, name="y_bf%d" % j, align_bytes=64) for j in range(chunks)]
+        y_codes = [sb.tile([P, WIDTHS[j]], U32, name="y_codes%d" % j, align_bytes=64) for j in range(chunks)]
+
+        def weave(j):
+            word = U32 if j == chunks - 1 else I32
+            dst = y_bf[j][:].rearrange("p c t -> p (c t)").bitcast(word).rearrange("p (c h) -> p c h", h=2)
+            src = pairs[j][:].rearrange("p h c e -> p (h c e)").bitcast(word).rearrange("p (h c) -> p c h", h=2)
+            if j == chunks - 1:
+                nc.scalar.copy(dst, src)
+            else:
+                nc.vector.tensor_copy(dst, src)
+
+        def quantise_out(j):
+            nc.vector.quantize_mx(
+                out=y_codes[j][:].bitcast(E4M3),
+                scales=y_scales[:, cols[j]],
+                in_=y_bf[j][:].rearrange("p c t -> p (c t)"),
+            )
+            nc.sync.dma_start(out_words[:, cols[j]], y_codes[j][:].bitcast(I32))
+
+        weave(0)
+        for j in range(1, chunks):
+            weave(j)
+            quantise_out(j - 1)
+        quantise_out(chunks - 1)
+        for quad in range(4):
+            queue = nc.sync if quad % 2 == 0 else nc.scalar
+            queue.dma_start(out_scales[4 * quad:4 * quad + 4, :], y_scales[32 * quad:32 * quad + 4, :].bitcast(I32))

@@ -19,6 +19,7 @@ D = 512
 N = 512
 T = 2048
 U = 1024
+STORE = 512
 WIDTHS = (256, 256, 512, 512, 256, 256)
 
 FLOPS = 2 * F * D * N
@@ -48,46 +49,55 @@ def tile_attend_gtucker_pl_kernel(tc, bT, cT, er, C, aoffs, boffs, coffs, out_0,
         half = D // 2
         core = [sb.tile([P, LANES, half], F32, name="core%d" % h) for h in range(2)]
 
+        def load_b(t):
+            nc.sync.dma_start(b_tab[t][:], b_rows[:, t, :])
+
+        def load_c(t):
+            nc.sync.dma_start(c_tab[t][:], c_rows[:, t, :])
+
+        def load_core(h):
+            nc.sync.dma_start(core[h][:], core_rows[:, :, h * half:(h + 1) * half])
+
         nc.sync.dma_start(b_list[:], boffs)
-        nc.sync.dma_start(b_tab[0][:], b_rows[:, 0, :])
+        load_b(0)
         nc.sync.dma_start(er_sb[:], er)
         nc.sync.dma_start(c_list[:], coffs)
-        nc.sync.dma_start(c_tab[0][:], c_rows[:, 0, :])
         for t in range(1, LANES):
-            if t >= 2:
-                h = t - 2
-                nc.sync.dma_start(core[h][:], core_rows[:, :, h * half:(h + 1) * half])
-            nc.sync.dma_start(b_tab[t][:], b_rows[:, t, :])
-            nc.sync.dma_start(c_tab[t][:], c_rows[:, t, :])
+            load_b(t)
+            load_c(t - 1)
+        load_core(0)
+        load_c(LANES - 1)
+        load_core(1)
         nc.sync.dma_start(a_list[:], aoffs)
 
         window = [None] * LANES
-        for t in range(3):
-            window[t] = sb.tile([P, T], F32, name="window%d" % t)
-            nc.vector.memset(window[t][:].bitcast(I32), 0)
-
-        q_bf = sb.tile([P, N, LANES], BF16, name="q_bf", tag="q_bf", align_bytes=64)
-        q_pair = [sb.tile([P, 2, N], F32, name="q_pair%d" % h) for h in range(2)]
-        eb = [sb.tile([P, N], F32, name="eb%d" % h) for h in range(2)]
         for t in range(LANES):
+            window[t] = sb.tile([P, T], F32, name="window%d" % t)
+            nc.gpsimd.memset(window[t][:].bitcast(I32), 0)
+
+        q_bf = sb.tile([P, N, LANES], BF16, name="q_bf", align_bytes=64)
+        q_pair = [sb.tile([P, 2, N], F32, name="q_pair%d" % h) for h in range(2)]
+        eb = [sb.tile([P, N], F32, name="eb%d" % t) for t in range(LANES)]
+
+        def gather_b(t):
+            nc.vector.tensor_tensor(eb[t][:], b_tab[t][:].indirect(b_list[:]), er_sb[:], MULT)
+
+        def gather_c(t):
             h, e = divmod(t, 2)
-            nc.vector.tensor_tensor(eb[e][:], b_tab[t][:].indirect(b_list[:]), er_sb[:], MULT)
-            nc.vector.tensor_tensor(q_pair[h][:, e, :], c_tab[t][:].indirect(c_list[:]), eb[e][:], MULT)
-            if t == 1:
-                nc.scalar.copy(q_bf[:, :, 0:2], q_pair[0][:].rearrange("p e i -> p i e"))
-        nc.vector.tensor_copy(q_bf[:, :, 2:4], q_pair[1][:].rearrange("p e i -> p i e"))
+            nc.vector.tensor_tensor(q_pair[h][:, e, :], c_tab[t][:].indirect(c_list[:]), eb[t][:], MULT)
 
         core_bf = sb.tile([P, LANES, P, LANES], BF16, name="core_bf", align_bytes=64)
-        mh = P // 2
-        for h in range(2):
-            nc.scalar.copy(
-                core_bf[:, :, h * mh:(h + 1) * mh, :].rearrange("p t m j -> p m j t"),
-                core[h][:].rearrange("p j (m t) -> p m j t", t=LANES),
-            )
         core_codes = sb.tile([P, LANES, P], U32, name="core_codes", align_bytes=64)
         core_scales = sb.tile([P, LANES, P], U8, name="core_scales", align_bytes=64)
         q_codes = sb.tile([P, N], U32, name="q_codes", align_bytes=64)
         q_scales = sb.tile([P, N], U8, name="q_scales", align_bytes=64)
+        mh = P // 2
+
+        def deal_core(h, first, last):
+            nc.scalar.copy(
+                core_bf[:, first:last, h * mh:(h + 1) * mh, :].rearrange("p t m j -> p m j t"),
+                core[h][:].rearrange("p j (m t) -> p m j t", t=LANES)[:, :, :, first:last],
+            )
 
         def quantise_core(t):
             nc.vector.quantize_mx(
@@ -96,12 +106,24 @@ def tile_attend_gtucker_pl_kernel(tc, bT, cT, er, C, aoffs, boffs, coffs, out_0,
                 in_=core_bf[:, t, :, :].rearrange("p m j -> p (m j)"),
             )
 
-        quantise_core(0)
-        nc.vector.quantize_mx(out=q_codes[:].bitcast(E5M2), scales=q_scales[:], in_=q_bf[:].rearrange("p i t -> p (i t)"))
+        gather_b(0)
         for t in range(1, LANES):
+            gather_b(t)
+            gather_c(t - 1)
+            if t == 2:
+                nc.scalar.copy(q_bf[:, :, 0:2], q_pair[0][:].rearrange("p e i -> p i e"))
+        gather_c(LANES - 1)
+        deal_core(0, 0, LANES)
+        deal_core(1, 0, LANES)
+        hn = N // 2
+        for r in range(2):
+            run = slice(r * hn, (r + 1) * hn)
+            nc.vector.tensor_copy(q_bf[:, run, 2:4], q_pair[1][:, :, run].rearrange("p e i -> p i e"))
+        for r in range(2):
+            run = slice(r * hn, (r + 1) * hn)
+            nc.vector.quantize_mx(out=q_codes[:, run].bitcast(E5M2), scales=q_scales[:, run], in_=q_bf[:, run, :].rearrange("p i t -> p (i t)"))
+        for t in range(LANES):
             quantise_core(t)
-        window[3] = sb.tile([P, T], F32, name="window3", tag="q_bf", align_bytes=64)
-        nc.vector.memset(window[3][:].bitcast(I32), 0)
 
         da = []
         for t in range(LANES):
@@ -116,39 +138,44 @@ def tile_attend_gtucker_pl_kernel(tc, bT, cT, er, C, aoffs, boffs, coffs, out_0,
                 stop=True,
             )
             da_t = sb.tile([P, N], F32, name="da%d" % t)
-            nc.scalar.copy(da_t[:], acc[:])
+            if t == 0:
+                nc.vector.tensor_copy(da_t[:], acc[:])
+            else:
+                nc.scalar.copy(da_t[:], acc[:])
             da.append(da_t)
 
         chunks = len(WIDTHS)
         cols = [slice(sum(WIDTHS[:j]), sum(WIDTHS[:j + 1])) for j in range(chunks)]
-        pairs = [sb.tile([P, 2, WIDTHS[j], 2], BF16, name="pairs%d" % j, align_bytes=64) for j in range(chunks)]
+        pairs = sb.tile([P, 2, T, 2], BF16, name="pairs", align_bytes=64)
         for t in range(LANES):
             h, e = divmod(t, 2)
             nc.vector.tensor_copy(window[t][:].indirect(a_list[:]), da[t][:])
             nc.sync.dma_start(out_rows[:, t, :], window[t][:])
-            for j in range(chunks):
-                nc.scalar.copy(pairs[j][:, h, :, e], window[t][:, cols[j]])
+            for run in (cols if t == LANES - 1 else [slice(0, T)]):
+                nc.scalar.copy(pairs[:, h, run, e], window[t][:, run])
 
         y_scales = sb.tile([P, T], U8, name="y_scales", align_bytes=64)
+        y_codes = [sb.tile([P, STORE], U32, name="y_codes%d" % s, align_bytes=64) for s in range(T // STORE)]
         y_bf = [sb.tile([P, WIDTHS[j], LANES], BF16, name="y_bf%d" % j, align_bytes=64) for j in range(chunks)]
-        y_codes = [sb.tile([P, WIDTHS[j]], U32, name="y_codes%d" % j, align_bytes=64) for j in range(chunks)]
 
         def weave(j):
-            word = U32 if j == chunks - 1 else I32
+            word = U32 if j >= chunks - 2 else I32
             dst = y_bf[j][:].rearrange("p c t -> p (c t)").bitcast(word).rearrange("p (c h) -> p c h", h=2)
-            src = pairs[j][:].rearrange("p h c e -> p (h c e)").bitcast(word).rearrange("p (h c) -> p c h", h=2)
-            if j == chunks - 1:
+            src = pairs[:].rearrange("p h c e -> p (h c e)").bitcast(word).rearrange("p (h c) -> p c h", h=2)[:, cols[j], :]
+            if j >= chunks - 2:
                 nc.scalar.copy(dst, src)
             else:
                 nc.vector.tensor_copy(dst, src)
 
         def quantise_out(j):
+            s, first = divmod(cols[j].start, STORE)
             nc.vector.quantize_mx(
-                out=y_codes[j][:].bitcast(E4M3),
+                out=y_codes[s][:, first:first + WIDTHS[j]].bitcast(E4M3),
                 scales=y_scales[:, cols[j]],
                 in_=y_bf[j][:].rearrange("p c t -> p (c t)"),
             )
-            nc.sync.dma_start(out_words[:, cols[j]], y_codes[j][:].bitcast(I32))
+            if cols[j].stop % STORE == 0:
+                nc.sync.dma_start(out_words[:, s * STORE:(s + 1) * STORE], y_codes[s][:].bitcast(I32))
 
         weave(0)
         for j in range(1, chunks):
@@ -156,5 +183,5 @@ def tile_attend_gtucker_pl_kernel(tc, bT, cT, er, C, aoffs, boffs, coffs, out_0,
             quantise_out(j - 1)
         quantise_out(chunks - 1)
         for quad in range(4):
-            queue = nc.sync if quad % 2 == 0 else nc.scalar
+            queue = nc.scalar if quad % 2 == 0 else nc.sync
             queue.dma_start(out_scales[4 * quad:4 * quad + 4, :], y_scales[32 * quad:32 * quad + 4, :].bitcast(I32))

@@ -1,6 +1,7 @@
 from contextlib import ExitStack
 
 import concourse.mybir as mybir
+from concourse.masks import make_identity
 
 F32 = mybir.dt.float32
 BF16 = mybir.dt.bfloat16
@@ -11,6 +12,7 @@ U8 = mybir.dt.uint8
 E4M3 = mybir.dt.float8_e4m3fn_x4
 E5M2 = mybir.dt.float8_e5m2_x4
 MULT = mybir.AluOpType.mult
+COPY = mybir.ActivationFunctionType.Copy
 
 P = 128
 LANES = 4
@@ -20,6 +22,8 @@ N = 512
 T = 2048
 U = 1024
 STORE = 512
+CORE_WIDTHS = (128, 192, 192)
+B_ORDER = (2, 3, 0, 1)
 WIDTHS = (256, 256, 512, 512, 256, 256)
 
 FLOPS = 2 * F * D * N
@@ -43,11 +47,13 @@ def tile_attend_gtucker_pl_kernel(tc, bT, cT, er, C, aoffs, boffs, coffs, out_0,
         out_words = out_1[0].rearrange("p c l -> p (c l)").bitcast(I32)
         out_scales = out_2[0].bitcast(I32)
 
-        b_tab = [sb.tile([P, U], F32, name="b_tab%d" % t) for t in range(LANES)]
+        b_tab = [sb.tile([P, U], F32, name="b_tab%d" % t, tag="b_tab%d" % t) for t in range(LANES)]
         c_tab = [sb.tile([P, U], F32, name="c_tab%d" % t) for t in range(LANES)]
         er_sb = sb.tile([P, N], F32, name="er_sb")
-        half = D // 2
-        core = [sb.tile([P, LANES, half], F32, name="core%d" % h) for h in range(2)]
+        blocks = N // P
+        er_col = sb.tile([P, blocks], F32, name="er_col")
+        core = [sb.tile([P, LANES, w], F32, name="core%d" % h) for h, w in enumerate(CORE_WIDTHS)]
+        core_first = [sum(CORE_WIDTHS[:h]) for h in range(len(CORE_WIDTHS))]
 
         def load_b(t):
             nc.sync.dma_start(b_tab[t][:], b_rows[:, t, :])
@@ -56,46 +62,66 @@ def tile_attend_gtucker_pl_kernel(tc, bT, cT, er, C, aoffs, boffs, coffs, out_0,
             nc.sync.dma_start(c_tab[t][:], c_rows[:, t, :])
 
         def load_core(h):
-            nc.sync.dma_start(core[h][:], core_rows[:, :, h * half:(h + 1) * half])
+            nc.sync.dma_start(core[h][:], core_rows[:, :, core_first[h]:core_first[h] + CORE_WIDTHS[h]])
 
         nc.sync.dma_start(b_list[:], boffs)
-        load_b(0)
-        nc.sync.dma_start(er_sb[:], er)
-        nc.sync.dma_start(c_list[:], coffs)
-        for t in range(1, LANES):
+        load_b(B_ORDER[0])
+        with nc.allow_non_contiguous_dma(reason="one error a partition"):
+            nc.sync.dma_start(er_col[:], er[0].rearrange("(k p) -> p k", p=P))
+        for t in B_ORDER[1:]:
             load_b(t)
-            load_c(t - 1)
+        nc.sync.dma_start(c_list[:], coffs)
         load_core(0)
-        load_c(LANES - 1)
+        for t in range(LANES):
+            load_c(t)
         load_core(1)
+        load_core(2)
         nc.sync.dma_start(a_list[:], aoffs)
 
+        ident = sb.tile([P, P], F32, name="ident")
+        make_identity(nc, ident[:])
         window = [None] * LANES
-        for t in range(LANES):
-            window[t] = sb.tile([P, T], F32, name="window%d" % t)
-            nc.gpsimd.memset(window[t][:].bitcast(I32), 0)
+        window[0] = sb.tile([P, T], F32, name="window0")
+        nc.gpsimd.memset(window[0][:].bitcast(I32), 0)
 
         q_bf = sb.tile([P, N, LANES], BF16, name="q_bf", align_bytes=64)
         q_pair = [sb.tile([P, 2, N], F32, name="q_pair%d" % h) for h in range(2)]
         eb = [sb.tile([P, N], F32, name="eb%d" % t) for t in range(LANES)]
 
+        er_ps = psum.tile([P, blocks, P], F32, name="er_ps", tag="acc3")
+        for k in range(blocks):
+            nc.tensor.transpose(er_ps[:, k, :], er_col[:, k:k + 1].to_broadcast([P, P]), ident[:])
+        nc.scalar.copy(er_sb[:], er_ps[:].rearrange("p k n -> p (k n)"))
+
         def gather_b(t):
-            nc.vector.tensor_tensor(eb[t][:], b_tab[t][:].indirect(b_list[:]), er_sb[:], MULT)
+            if t < 2:
+                nc.vector.tensor_tensor(eb[t][:], b_tab[t][:].indirect(b_list[:]), er_sb[:], MULT)
+                return
+            plain = sb.tile([P, N], F32, name="plain%d" % t)
+            nc.vector.tensor_copy(plain[:], b_tab[t][:].indirect(b_list[:]))
+            turned_ps = psum.tile([P, blocks, P], F32, name="turned_ps", tag="turned_ps", bufs=2)
+            for k in range(blocks):
+                nc.tensor.transpose(turned_ps[:, k, :], plain[:, k * P:(k + 1) * P], ident[:])
+            turned = sb.tile([P, blocks, P], F32, name="turned%d" % t, tag="turned%d" % t, align_bytes=64)
+            for k in range(blocks):
+                nc.scalar.activation(turned[:, k, :], turned_ps[:, k, :], COPY, scale=er_col[:, k:k + 1])
+            back_ps = psum.tile([P, blocks, P], F32, name="back_ps", tag="back_ps", bufs=2)
+            for k in range(blocks):
+                nc.tensor.transpose(back_ps[:, k, :], turned[:, k, :], ident[:])
+            nc.scalar.copy(eb[t][:], back_ps[:].rearrange("p k n -> p (k n)"))
 
         def gather_c(t):
             h, e = divmod(t, 2)
             nc.vector.tensor_tensor(q_pair[h][:, e, :], c_tab[t][:].indirect(c_list[:]), eb[t][:], MULT)
 
-        core_bf = sb.tile([P, LANES, P, LANES], BF16, name="core_bf", align_bytes=64)
         core_codes = sb.tile([P, LANES, P], U32, name="core_codes", align_bytes=64)
         core_scales = sb.tile([P, LANES, P], U8, name="core_scales", align_bytes=64)
         q_codes = sb.tile([P, N], U32, name="q_codes", align_bytes=64)
         q_scales = sb.tile([P, N], U8, name="q_scales", align_bytes=64)
-        mh = P // 2
 
         def deal_core(h, first, last):
             nc.scalar.copy(
-                core_bf[:, first:last, h * mh:(h + 1) * mh, :].rearrange("p t m j -> p m j t"),
+                core_bf[:, first:last, core_first[h] // LANES:(core_first[h] + CORE_WIDTHS[h]) // LANES, :].rearrange("p t m j -> p m j t"),
                 core[h][:].rearrange("p j (m t) -> p m j t", t=LANES)[:, :, :, first:last],
             )
 
@@ -106,15 +132,20 @@ def tile_attend_gtucker_pl_kernel(tc, bT, cT, er, C, aoffs, boffs, coffs, out_0,
                 in_=core_bf[:, t, :, :].rearrange("p m j -> p (m j)"),
             )
 
-        gather_b(0)
-        for t in range(1, LANES):
+        for t in B_ORDER:
             gather_b(t)
-            gather_c(t - 1)
-            if t == 2:
-                nc.scalar.copy(q_bf[:, :, 0:2], q_pair[0][:].rearrange("p e i -> p i e"))
-        gather_c(LANES - 1)
+        for t in range(1, LANES):
+            window[t] = sb.tile([P, T], F32, name="window%d" % t, tag="b_tab%d" % B_ORDER[t])
+            nc.gpsimd.memset(window[t][:].bitcast(I32), 0)
+        core_bf = sb.tile([P, LANES, P, LANES], BF16, name="core_bf", tag="turned3", align_bytes=64)
         deal_core(0, 0, LANES)
+        for t in range(LANES):
+            gather_c(t)
+            if t == 1:
+                nc.scalar.copy(q_bf[:, :, 0:2], q_pair[0][:].rearrange("p e i -> p i e"))
         deal_core(1, 0, LANES)
+        deal_core(2, 0, 1)
+        deal_core(2, 1, LANES)
         hn = N // 2
         for r in range(2):
             run = slice(r * hn, (r + 1) * hn)
@@ -127,7 +158,7 @@ def tile_attend_gtucker_pl_kernel(tc, bT, cT, er, C, aoffs, boffs, coffs, out_0,
 
         da = []
         for t in range(LANES):
-            acc = psum.tile([P, N], F32, name="acc%d" % t)
+            acc = psum.tile([P, N], F32, name="acc%d" % t, tag="acc%d" % t)
             nc.tensor.matmul_mx(
                 out=acc[:],
                 lhsT=core_codes[:, t, :].bitcast(E4M3),

@@ -183,7 +183,10 @@ def tile_attend_gtucker_pl_kernel(tc, bT, cT, er, C, aoffs, boffs, coffs, out_0,
             nc.vector.tensor_copy(window[t][:].indirect(a_list[:]), da[t][:])
             nc.sync.dma_start(out_rows[:, t, :], window[t][:])
             for run in (cols if t == LANES - 1 else [slice(0, T)]):
-                nc.scalar.copy(pairs[:, h, run, e], window[t][:, run])
+                if t < 2:
+                    nc.gpsimd.tensor_copy(pairs[:, h, run, e], window[t][:, run])
+                else:
+                    nc.scalar.copy(pairs[:, h, run, e], window[t][:, run])
 
         y_scales = sb.tile([P, T], U8, name="y_scales", align_bytes=64)
         y_codes = [sb.tile([P, STORE], U32, name="y_codes%d" % s, align_bytes=64) for s in range(T // STORE)]

@@ -21,10 +21,10 @@ D = 512
 N = 512
 T = 2048
 U = 1024
-STORE = 512
+STORES = (1024, 768, 256)
 CORE_WIDTHS = (128, 192, 192)
 B_ORDER = (2, 3, 0, 1)
-WIDTHS = (256, 256, 512, 512, 256, 256)
+WIDTHS = (512, 512, 512, 256, 256)
 
 FLOPS = 2 * F * D * N
 
@@ -175,47 +175,42 @@ def tile_attend_gtucker_pl_kernel(tc, bT, cT, er, C, aoffs, boffs, coffs, out_0,
                 nc.scalar.copy(da_t[:], acc[:])
             da.append(da_t)
 
-        chunks = len(WIDTHS)
-        cols = [slice(sum(WIDTHS[:j]), sum(WIDTHS[:j + 1])) for j in range(chunks)]
-        pairs = sb.tile([P, 2, T, 2], BF16, name="pairs", align_bytes=64)
+        half = T // 2
+        y_bf = [sb.tile([P, half, LANES], BF16, name="y_bf%d" % h, align_bytes=64) for h in range(2)]
+        y_scales = sb.tile([P, T], U8, name="y_scales", align_bytes=64)
+        y_codes = [sb.tile([P, w], U32, name="y_codes%d" % s, align_bytes=64) for s, w in enumerate(STORES)]
+        stored = [slice(sum(STORES[:s]), sum(STORES[:s + 1])) for s in range(len(STORES))]
+        last = LANES - 1
         for t in range(LANES):
-            h, e = divmod(t, 2)
             nc.vector.tensor_copy(window[t][:].indirect(a_list[:]), da[t][:])
             nc.sync.dma_start(out_rows[:, t, :], window[t][:])
-            for run in (cols if t == LANES - 1 else [slice(0, T)]):
-                if t < 2:
-                    nc.gpsimd.tensor_copy(pairs[:, h, run, e], window[t][:, run])
-                else:
-                    nc.scalar.copy(pairs[:, h, run, e], window[t][:, run])
+            if t < last - 1:
+                nc.gpsimd.tensor_copy(y_bf[0][:, :, t], window[t][:, 0:half])
+            if t == last - 1:
+                nc.gpsimd.tensor_copy(y_bf[0][:, :, t:t + 2], window[t][:, 0:half].unsqueeze(2).to_broadcast([P, half, 2]))
+            if t < last:
+                nc.scalar.copy(y_bf[1][:, :, t], window[t][:, half:T])
 
-        y_scales = sb.tile([P, T], U8, name="y_scales", align_bytes=64)
-        y_codes = [sb.tile([P, STORE], U32, name="y_codes%d" % s, align_bytes=64) for s in range(T // STORE)]
-        y_bf = [sb.tile([P, WIDTHS[j], LANES], BF16, name="y_bf%d" % j, align_bytes=64) for j in range(chunks)]
-
-        def weave(j):
-            word = U32 if j >= chunks - 2 else I32
-            dst = y_bf[j][:].rearrange("p c t -> p (c t)").bitcast(word).rearrange("p (c h) -> p c h", h=2)
-            src = pairs[:].rearrange("p h c e -> p (h c e)").bitcast(word).rearrange("p (h c) -> p c h", h=2)[:, cols[j], :]
-            if j >= chunks - 2:
-                nc.scalar.copy(dst, src)
+        cols = [slice(sum(WIDTHS[:j]), sum(WIDTHS[:j + 1])) for j in range(len(WIDTHS))]
+        for run in cols:
+            h, first = divmod(run.start, half)
+            dst = y_bf[h][:, first:first + run.stop - run.start, last]
+            if h == 0:
+                nc.vector.tensor_copy(dst, window[last][:, run])
             else:
-                nc.vector.tensor_copy(dst, src)
-
-        def quantise_out(j):
-            s, first = divmod(cols[j].start, STORE)
+                nc.scalar.copy(dst, window[last][:, run])
+        for run in cols:
+            h, first = divmod(run.start, half)
+            width = run.stop - run.start
+            s = [k for k in range(len(STORES)) if stored[k].start <= run.start][-1]
+            word = run.start - stored[s].start
             nc.vector.quantize_mx(
-                out=y_codes[s][:, first:first + WIDTHS[j]].bitcast(E4M3),
-                scales=y_scales[:, cols[j]],
-                in_=y_bf[j][:].rearrange("p c t -> p (c t)"),
+                out=y_codes[s][:, word:word + width].bitcast(E4M3),
+                scales=y_scales[:, run],
+                in_=y_bf[h][:, first:first + width, :].rearrange("p c t -> p (c t)"),
             )
-            if cols[j].stop % STORE == 0:
-                nc.sync.dma_start(out_words[:, s * STORE:(s + 1) * STORE], y_codes[s][:].bitcast(I32))
-
-        weave(0)
-        for j in range(1, chunks):
-            weave(j)
-            quantise_out(j - 1)
-        quantise_out(chunks - 1)
+            if run.stop == stored[s].stop:
+                nc.sync.dma_start(out_words[:, stored[s]], y_codes[s][:].bitcast(I32))
         for quad in range(4):
             queue = nc.scalar if quad % 2 == 0 else nc.sync
             queue.dma_start(out_scales[4 * quad:4 * quad + 4, :], y_scales[32 * quad:32 * quad + 4, :].bitcast(I32))

@@ -1,7 +1,6 @@
 from contextlib import ExitStack
 
 import concourse.mybir as mybir
-from concourse.masks import make_identity
 
 F32 = mybir.dt.float32
 BF16 = mybir.dt.bfloat16
@@ -12,7 +11,6 @@ U8 = mybir.dt.uint8
 E4M3 = mybir.dt.float8_e4m3fn_x4
 E5M2 = mybir.dt.float8_e5m2_x4
 MULT = mybir.AluOpType.mult
-COPY = mybir.ActivationFunctionType.Copy
 
 P = 128
 LANES = 4
@@ -21,10 +19,9 @@ D = 512
 N = 512
 T = 2048
 U = 1024
-STORES = (1024, 768, 256)
-CORE_WIDTHS = (128, 192, 192)
-B_ORDER = (2, 3, 0, 1)
-WIDTHS = (512, 512, 512, 256, 256)
+STORES = (768, 768, 512)
+CORE_WIDTHS = (128, 256, 128)
+WIDTHS = (512, 256, 256, 512, 256, 256)
 
 FLOPS = 2 * F * D * N
 
@@ -47,11 +44,9 @@ def tile_attend_gtucker_pl_kernel(tc, bT, cT, er, C, aoffs, boffs, coffs, out_0,
         out_words = out_1[0].rearrange("p c l -> p (c l)").bitcast(I32)
         out_scales = out_2[0].bitcast(I32)
 
-        b_tab = [sb.tile([P, U], F32, name="b_tab%d" % t, tag="b_tab%d" % t) for t in range(LANES)]
+        b_tab = [sb.tile([P, U], F32, name="b_tab%d" % t) for t in range(LANES)]
         c_tab = [sb.tile([P, U], F32, name="c_tab%d" % t) for t in range(LANES)]
         er_sb = sb.tile([P, N], F32, name="er_sb")
-        blocks = N // P
-        er_col = sb.tile([P, blocks], F32, name="er_col")
         core = [sb.tile([P, LANES, w], F32, name="core%d" % h) for h, w in enumerate(CORE_WIDTHS)]
         core_first = [sum(CORE_WIDTHS[:h]) for h in range(len(CORE_WIDTHS))]
 
@@ -65,95 +60,81 @@ def tile_attend_gtucker_pl_kernel(tc, bT, cT, er, C, aoffs, boffs, coffs, out_0,
             nc.sync.dma_start(core[h][:], core_rows[:, :, core_first[h]:core_first[h] + CORE_WIDTHS[h]])
 
         nc.sync.dma_start(b_list[:], boffs)
-        load_b(B_ORDER[0])
-        with nc.allow_non_contiguous_dma(reason="one error a partition"):
-            nc.sync.dma_start(er_col[:], er[0].rearrange("(k p) -> p k", p=P))
-        for t in B_ORDER[1:]:
-            load_b(t)
+        nc.sync.dma_start(er_sb[:], er)
+        load_b(0)
+        load_b(1)
         nc.sync.dma_start(c_list[:], coffs)
+        load_c(0)
+        load_c(1)
+        load_b(2)
+        load_b(3)
         load_core(0)
-        for t in range(LANES):
-            load_c(t)
+        load_c(2)
+        load_c(3)
         load_core(1)
         load_core(2)
         nc.sync.dma_start(a_list[:], aoffs)
 
-        ident = sb.tile([P, P], F32, name="ident")
-        make_identity(nc, ident[:])
-        window = [None] * LANES
-        window[0] = sb.tile([P, T], F32, name="window0")
-        nc.gpsimd.memset(window[0][:].bitcast(I32), 0)
+        window = [sb.tile([P, T], F32, name="window%d" % t) for t in range(LANES)]
+        for t in range(LANES):
+            nc.gpsimd.memset(window[t][:].bitcast(I32), 0)
 
         q_bf = sb.tile([P, N, LANES], BF16, name="q_bf", align_bytes=64)
-        q_pair = [sb.tile([P, 2, N], F32, name="q_pair%d" % h) for h in range(2)]
-        eb = [sb.tile([P, N], F32, name="eb%d" % t) for t in range(LANES)]
-
-        er_ps = psum.tile([P, blocks, P], F32, name="er_ps", tag="acc3")
-        for k in range(blocks):
-            nc.tensor.transpose(er_ps[:, k, :], er_col[:, k:k + 1].to_broadcast([P, P]), ident[:])
-        nc.scalar.copy(er_sb[:], er_ps[:].rearrange("p k n -> p (k n)"))
+        q_pair = [sb.tile([P, 2, N], F32, name="q_pair%d" % h, tag="q_pair%d" % h, align_bytes=64) for h in range(2)]
+        eb = [sb.tile([P, N], F32, name="eb%d" % t, tag="eb%d" % t, align_bytes=64) for t in range(LANES)]
 
         def gather_b(t):
-            if t < 2:
-                nc.vector.tensor_tensor(eb[t][:], b_tab[t][:].indirect(b_list[:]), er_sb[:], MULT)
-                return
-            plain = sb.tile([P, N], F32, name="plain%d" % t)
-            nc.vector.tensor_copy(plain[:], b_tab[t][:].indirect(b_list[:]))
-            turned_ps = psum.tile([P, blocks, P], F32, name="turned_ps", tag="turned_ps", bufs=2)
-            for k in range(blocks):
-                nc.tensor.transpose(turned_ps[:, k, :], plain[:, k * P:(k + 1) * P], ident[:])
-            turned = sb.tile([P, blocks, P], F32, name="turned%d" % t, tag="turned%d" % t, align_bytes=64)
-            for k in range(blocks):
-                nc.scalar.activation(turned[:, k, :], turned_ps[:, k, :], COPY, scale=er_col[:, k:k + 1])
-            back_ps = psum.tile([P, blocks, P], F32, name="back_ps", tag="back_ps", bufs=2)
-            for k in range(blocks):
-                nc.tensor.transpose(back_ps[:, k, :], turned[:, k, :], ident[:])
-            nc.scalar.copy(eb[t][:], back_ps[:].rearrange("p k n -> p (k n)"))
+            nc.vector.tensor_tensor(eb[t][:], b_tab[t][:].indirect(b_list[:]), er_sb[:], MULT)
 
-        def gather_c(t):
+        def gather_c(t, run):
             h, e = divmod(t, 2)
-            nc.vector.tensor_tensor(q_pair[h][:, e, :], c_tab[t][:].indirect(c_list[:]), eb[t][:], MULT)
+            nc.vector.tensor_tensor(q_pair[h][:, e, run], c_tab[t][:].indirect(c_list[:, run.start // 16:run.stop // 16]), eb[t][:, run], MULT)
 
         core_codes = sb.tile([P, LANES, P], U32, name="core_codes", align_bytes=64)
         core_scales = sb.tile([P, LANES, P], U8, name="core_scales", align_bytes=64)
         q_codes = sb.tile([P, N], U32, name="q_codes", align_bytes=64)
         q_scales = sb.tile([P, N], U8, name="q_scales", align_bytes=64)
 
-        def deal_core(h, first, last):
+        def deal_core(h, tiles):
             nc.scalar.copy(
-                core_bf[:, first:last, core_first[h] // LANES:(core_first[h] + CORE_WIDTHS[h]) // LANES, :].rearrange("p t m j -> p m j t"),
-                core[h][:].rearrange("p j (m t) -> p m j t", t=LANES)[:, :, :, first:last],
+                core_bf[tiles.start][:, :, core_first[h] // LANES:(core_first[h] + CORE_WIDTHS[h]) // LANES, :].rearrange("p t m j -> p m j t"),
+                core[h][:].rearrange("p j (m t) -> p m j t", t=LANES)[:, :, :, tiles],
             )
 
         def quantise_core(t):
             nc.vector.quantize_mx(
                 out=core_codes[:, t, :].bitcast(E4M3),
                 scales=core_scales[:, t, :],
-                in_=core_bf[:, t, :, :].rearrange("p m j -> p (m j)"),
+                in_=core_bf[min(t, 1)][:, max(t - 1, 0), :, :].rearrange("p m j -> p (m j)"),
             )
 
-        for t in B_ORDER:
-            gather_b(t)
-        for t in range(1, LANES):
-            window[t] = sb.tile([P, T], F32, name="window%d" % t, tag="b_tab%d" % B_ORDER[t])
-            nc.gpsimd.memset(window[t][:].bitcast(I32), 0)
-        core_bf = sb.tile([P, LANES, P, LANES], BF16, name="core_bf", tag="turned3", align_bytes=64)
-        deal_core(0, 0, LANES)
-        for t in range(LANES):
-            gather_c(t)
-            if t == 1:
-                nc.scalar.copy(q_bf[:, :, 0:2], q_pair[0][:].rearrange("p e i -> p i e"))
-        deal_core(1, 0, LANES)
-        deal_core(2, 0, 1)
-        deal_core(2, 1, LANES)
         hn = N // 2
-        for r in range(2):
-            run = slice(r * hn, (r + 1) * hn)
+        halves = [slice(0, hn), slice(hn, N)]
+        gather_b(0)
+        gather_b(1)
+        gather_c(0, slice(0, N))
+        gather_c(1, slice(0, N))
+        nc.scalar.copy(q_bf[:, :, 0:2], q_pair[0][:].rearrange("p e i -> p i e"))
+        gather_b(2)
+        gather_b(3)
+        gather_c(2, slice(0, N))
+        for run in halves:
+            gather_c(3, run)
+        core_bf = [sb.tile([P, w, P, LANES], BF16, name="core_bf%d" % k, tag=("eb0", "q_pair0")[k], align_bytes=64) for k, w in enumerate((1, LANES - 1))]
+        first_tile, other_tiles = slice(0, 1), slice(1, LANES)
+        deal_core(0, first_tile)
+        deal_core(0, other_tiles)
+        deal_core(1, first_tile)
+        deal_core(2, first_tile)
+        deal_core(1, other_tiles)
+        deal_core(2, other_tiles)
+        for run in halves:
             nc.vector.tensor_copy(q_bf[:, run, 2:4], q_pair[1][:, :, run].rearrange("p e i -> p i e"))
-        for r in range(2):
-            run = slice(r * hn, (r + 1) * hn)
+        for r, run in enumerate(halves):
             nc.vector.quantize_mx(out=q_codes[:, run].bitcast(E5M2), scales=q_scales[:, run], in_=q_bf[:, run, :].rearrange("p i t -> p (i t)"))
-        for t in range(LANES):
+            if r == 0:
+                quantise_core(0)
+        for t in range(1, LANES):
             quantise_core(t)
 
         da = []
@@ -177,7 +158,7 @@ def tile_attend_gtucker_pl_kernel(tc, bT, cT, er, C, aoffs, boffs, coffs, out_0,
 
         half = T // 2
         y_bf = [sb.tile([P, half, LANES], BF16, name="y_bf%d" % h, align_bytes=64) for h in range(2)]
-        y_scales = sb.tile([P, T], U8, name="y_scales", align_bytes=64)
+        y_scales = sb.tile([P, half], U8, name="y_scales", align_bytes=64)
         y_codes = [sb.tile([P, w], U32, name="y_codes%d" % s, align_bytes=64) for s, w in enumerate(STORES)]
         stored = [slice(sum(STORES[:s]), sum(STORES[:s + 1])) for s in range(len(STORES))]
         last = LANES - 1
@@ -206,11 +187,11 @@ def tile_attend_gtucker_pl_kernel(tc, bT, cT, er, C, aoffs, boffs, coffs, out_0,
             word = run.start - stored[s].start
             nc.vector.quantize_mx(
                 out=y_codes[s][:, word:word + width].bitcast(E4M3),
-                scales=y_scales[:, run],
+                scales=y_scales[LANES * h:P, first:first + width],
                 in_=y_bf[h][:, first:first + width, :].rearrange("p c t -> p (c t)"),
             )
             if run.stop == stored[s].stop:
                 nc.sync.dma_start(out_words[:, stored[s]], y_codes[s][:].bitcast(I32))
         for quad in range(4):
             queue = nc.scalar if quad % 2 == 0 else nc.sync
-            queue.dma_start(out_scales[4 * quad:4 * quad + 4, :], y_scales[32 * quad:32 * quad + 4, :].bitcast(I32))
+            queue.dma_start(out_scales[4 * quad:4 * quad + 4, :].rearrange("r (h x) -> h r x", h=2), y_scales[32 * quad:32 * quad + 8, :].bitcast(I32))

@@ -68,9 +68,9 @@ def tile_attend_gtucker_pl_kernel(tc, bT, cT, er, C, aoffs, boffs, coffs, out_0,
         load_c(1)
         load_b(2)
         load_b(3)
-        load_core(0)
         load_c(2)
         load_c(3)
+        load_core(0)
         load_core(1)
         load_core(2)
         nc.sync.dma_start(a_list[:], aoffs)

@@ -22,6 +22,10 @@ U = 1024
 STORES = (768, 768, 512)
 CORE_WIDTHS = (128, 256, 128)
 WIDTHS = (512, 256, 256, 512, 256, 256)
+DIRECT = 768
+PAIRED = T - 2 * DIRECT
+VECTOR_RUNS = (512, 256)
+SCALAR_RUNS = (512, 256)
 
 FLOPS = 2 * F * D * N
 
@@ -162,24 +166,31 @@ def tile_attend_gtucker_pl_kernel(tc, bT, cT, er, C, aoffs, boffs, coffs, out_0,
         y_codes = [sb.tile([P, w], U32, name="y_codes%d" % s, align_bytes=64) for s, w in enumerate(STORES)]
         stored = [slice(sum(STORES[:s]), sum(STORES[:s + 1])) for s in range(len(STORES))]
         last = LANES - 1
+        pairs = sb.tile([P, 2, PAIRED, 2], BF16, name="pairs", align_bytes=64)
+        high = DIRECT + PAIRED
         for t in range(LANES):
             nc.vector.tensor_copy(window[t][:].indirect(a_list[:]), da[t][:])
             nc.sync.dma_start(out_rows[:, t, :], window[t][:])
             if t < last - 1:
-                nc.gpsimd.tensor_copy(y_bf[0][:, :, t], window[t][:, 0:half])
+                nc.gpsimd.tensor_copy(y_bf[0][:, 0:DIRECT, t], window[t][:, 0:DIRECT])
             if t == last - 1:
-                nc.gpsimd.tensor_copy(y_bf[0][:, :, t:t + 2], window[t][:, 0:half].unsqueeze(2).to_broadcast([P, half, 2]))
+                nc.gpsimd.tensor_copy(y_bf[0][:, 0:DIRECT, t:t + 2], window[t][:, 0:DIRECT].unsqueeze(2).to_broadcast([P, DIRECT, 2]))
+            nc.scalar.copy(pairs[:, t // 2, :, t % 2], window[t][:, DIRECT:high])
             if t < last:
-                nc.scalar.copy(y_bf[1][:, :, t], window[t][:, half:T])
+                nc.scalar.copy(y_bf[1][:, high - half:half, t], window[t][:, high:T])
 
+        first = 0
+        for width in VECTOR_RUNS:
+            nc.vector.tensor_copy(y_bf[0][:, first:first + width, last], window[last][:, first:first + width])
+            first = first + width
+        first = high
+        for width in SCALAR_RUNS:
+            nc.scalar.copy(y_bf[1][:, first - half:first - half + width, last], window[last][:, first:first + width])
+            first = first + width
+        woven = pairs[:].rearrange("p h c e -> p c h e")
+        nc.vector.tensor_copy(y_bf[0][:, DIRECT:half, :].rearrange("p c (h e) -> p c h e", h=2), woven[:, 0:half - DIRECT])
+        nc.vector.tensor_copy(y_bf[1][:, 0:high - half, :].rearrange("p c (h e) -> p c h e", h=2), woven[:, half - DIRECT:PAIRED])
         cols = [slice(sum(WIDTHS[:j]), sum(WIDTHS[:j + 1])) for j in range(len(WIDTHS))]
-        for run in cols:
-            h, first = divmod(run.start, half)
-            dst = y_bf[h][:, first:first + run.stop - run.start, last]
-            if h == 0:
-                nc.vector.tensor_copy(dst, window[last][:, run])
-            else:
-                nc.scalar.copy(dst, window[last][:, run])
         for run in cols:
             h, first = divmod(run.start, half)
             width = run.stop - run.start

@@ -11,6 +11,7 @@ U8 = mybir.dt.uint8
 E4M3 = mybir.dt.float8_e4m3fn_x4
 E5M2 = mybir.dt.float8_e5m2_x4
 MULT = mybir.AluOpType.mult
+ADD = mybir.AluOpType.add
 
 P = 128
 LANES = 4
@@ -20,7 +21,7 @@ N = 512
 T = 2048
 U = 1024
 STORES = (768, 768, 512)
-CORE_WIDTHS = (128, 256, 128)
+CORE_WIDTHS = (128, 192, 192)
 WIDTHS = (512, 256, 256, 512, 256, 256)
 DIRECT = 768
 PAIRED = T - 2 * DIRECT
@@ -72,9 +73,9 @@ def tile_attend_gtucker_pl_kernel(tc, bT, cT, er, C, aoffs, boffs, coffs, out_0,
         load_c(1)
         load_b(2)
         load_b(3)
+        load_core(0)
         load_c(2)
         load_c(3)
-        load_core(0)
         load_core(1)
         load_core(2)
         nc.sync.dma_start(a_list[:], aoffs)
@@ -99,17 +100,17 @@ def tile_attend_gtucker_pl_kernel(tc, bT, cT, er, C, aoffs, boffs, coffs, out_0,
         q_codes = sb.tile([P, N], U32, name="q_codes", align_bytes=64)
         q_scales = sb.tile([P, N], U8, name="q_scales", align_bytes=64)
 
-        def deal_core(h, tiles):
+        def deal_core(h):
             nc.scalar.copy(
-                core_bf[tiles.start][:, :, core_first[h] // LANES:(core_first[h] + CORE_WIDTHS[h]) // LANES, :].rearrange("p t m j -> p m j t"),
-                core[h][:].rearrange("p j (m t) -> p m j t", t=LANES)[:, :, :, tiles],
+                core_bf[:, :, core_first[h] // LANES:(core_first[h] + CORE_WIDTHS[h]) // LANES, :].rearrange("p t m j -> p m j t"),
+                core[h][:].rearrange("p j (m t) -> p m j t", t=LANES),
             )
 
         def quantise_core(t):
             nc.vector.quantize_mx(
                 out=core_codes[:, t, :].bitcast(E4M3),
                 scales=core_scales[:, t, :],
-                in_=core_bf[min(t, 1)][:, max(t - 1, 0), :, :].rearrange("p m j -> p (m j)"),
+                in_=core_bf[:, t, :, :].rearrange("p m j -> p (m j)"),
             )
 
         hn = N // 2
@@ -124,14 +125,9 @@ def tile_attend_gtucker_pl_kernel(tc, bT, cT, er, C, aoffs, boffs, coffs, out_0,
         gather_c(2, slice(0, N))
         for run in halves:
             gather_c(3, run)
-        core_bf = [sb.tile([P, w, P, LANES], BF16, name="core_bf%d" % k, tag=("eb0", "q_pair0")[k], align_bytes=64) for k, w in enumerate((1, LANES - 1))]
-        first_tile, other_tiles = slice(0, 1), slice(1, LANES)
-        deal_core(0, first_tile)
-        deal_core(0, other_tiles)
-        deal_core(1, first_tile)
-        deal_core(2, first_tile)
-        deal_core(1, other_tiles)
-        deal_core(2, other_tiles)
+        core_bf = sb.tile([P, LANES, P, LANES], BF16, name="core_bf", tag="q_pair0", align_bytes=64)
+        for h in range(len(CORE_WIDTHS)):
+            deal_core(h)
         for run in halves:
             nc.vector.tensor_copy(q_bf[:, run, 2:4], q_pair[1][:, :, run].rearrange("p e i -> p i e"))
         for r, run in enumerate(halves):
@@ -172,9 +168,9 @@ def tile_attend_gtucker_pl_kernel(tc, bT, cT, er, C, aoffs, boffs, coffs, out_0,
             nc.vector.tensor_copy(window[t][:].indirect(a_list[:]), da[t][:])
             nc.sync.dma_start(out_rows[:, t, :], window[t][:])
             if t < last - 1:
-                nc.gpsimd.tensor_copy(y_bf[0][:, 0:DIRECT, t], window[t][:, 0:DIRECT])
+                nc.gpsimd.tensor_scalar(y_bf[0][:, 0:DIRECT, t], window[t][:, 0:DIRECT], 1.0, -0.0, MULT, ADD)
             if t == last - 1:
-                nc.gpsimd.tensor_copy(y_bf[0][:, 0:DIRECT, t:t + 2], window[t][:, 0:DIRECT].unsqueeze(2).to_broadcast([P, DIRECT, 2]))
+                nc.gpsimd.tensor_scalar(y_bf[0][:, 0:DIRECT, t:t + 2], window[t][:, 0:DIRECT].unsqueeze(2).to_broadcast([P, DIRECT, 2]), 1.0, -0.0, MULT, ADD)
             nc.scalar.copy(pairs[:, t // 2, :, t % 2], window[t][:, DIRECT:high])
             if t < last:
                 nc.scalar.copy(y_bf[1][:, high - half:half, t], window[t][:, high:T])

@@ -11,7 +11,6 @@ U8 = mybir.dt.uint8
 E4M3 = mybir.dt.float8_e4m3fn_x4
 E5M2 = mybir.dt.float8_e5m2_x4
 MULT = mybir.AluOpType.mult
-ADD = mybir.AluOpType.add
 
 P = 128
 LANES = 4
@@ -21,8 +20,8 @@ N = 512
 T = 2048
 U = 1024
 STORES = (768, 768, 512)
-CORE_WIDTHS = (128, 192, 192)
-WIDTHS = (512, 256, 256, 512, 256, 256)
+CORE_PIECES = ((0, 0, 512), (1, 0, 256), (1, 256, 512))
+WIDTHS = (256,) * 8
 DIRECT = 768
 PAIRED = T - 2 * DIRECT
 VECTOR_RUNS = (512, 256)
@@ -52,8 +51,7 @@ def tile_attend_gtucker_pl_kernel(tc, bT, cT, er, C, aoffs, boffs, coffs, out_0,
         b_tab = [sb.tile([P, U], F32, name="b_tab%d" % t) for t in range(LANES)]
         c_tab = [sb.tile([P, U], F32, name="c_tab%d" % t) for t in range(LANES)]
         er_sb = sb.tile([P, N], F32, name="er_sb")
-        core = [sb.tile([P, LANES, w], F32, name="core%d" % h) for h, w in enumerate(CORE_WIDTHS)]
-        core_first = [sum(CORE_WIDTHS[:h]) for h in range(len(CORE_WIDTHS))]
+        core = [sb.tile([P, 2, stop - start], F32, name="core%d" % h) for h, (pair, start, stop) in enumerate(CORE_PIECES)]
 
         def load_b(t):
             nc.sync.dma_start(b_tab[t][:], b_rows[:, t, :])
@@ -62,7 +60,8 @@ def tile_attend_gtucker_pl_kernel(tc, bT, cT, er, C, aoffs, boffs, coffs, out_0,
             nc.sync.dma_start(c_tab[t][:], c_rows[:, t, :])
 
         def load_core(h):
-            nc.sync.dma_start(core[h][:], core_rows[:, :, core_first[h]:core_first[h] + CORE_WIDTHS[h]])
+            pair, start, stop = CORE_PIECES[h]
+            nc.sync.dma_start(core[h][:], core_rows[:, 2 * pair:2 * pair + 2, start:stop])
 
         nc.sync.dma_start(b_list[:], boffs)
         nc.sync.dma_start(er_sb[:], er)
@@ -101,8 +100,9 @@ def tile_attend_gtucker_pl_kernel(tc, bT, cT, er, C, aoffs, boffs, coffs, out_0,
         q_scales = sb.tile([P, N], U8, name="q_scales", align_bytes=64)
 
         def deal_core(h):
+            pair, start, stop = CORE_PIECES[h]
             nc.scalar.copy(
-                core_bf[:, :, core_first[h] // LANES:(core_first[h] + CORE_WIDTHS[h]) // LANES, :].rearrange("p t m j -> p m j t"),
+                core_bf[:, :, start // LANES:stop // LANES, 2 * pair:2 * pair + 2].rearrange("p t m j -> p m j t"),
                 core[h][:].rearrange("p j (m t) -> p m j t", t=LANES),
             )
 
@@ -126,7 +126,7 @@ def tile_attend_gtucker_pl_kernel(tc, bT, cT, er, C, aoffs, boffs, coffs, out_0,
         for run in halves:
             gather_c(3, run)
         core_bf = sb.tile([P, LANES, P, LANES], BF16, name="core_bf", tag="q_pair0", align_bytes=64)
-        for h in range(len(CORE_WIDTHS)):
+        for h in range(len(CORE_PIECES)):
             deal_core(h)
         for run in halves:
             nc.vector.tensor_copy(q_bf[:, run, 2:4], q_pair[1][:, :, run].rearrange("p e i -> p i e"))
@@ -158,7 +158,7 @@ def tile_attend_gtucker_pl_kernel(tc, bT, cT, er, C, aoffs, boffs, coffs, out_0,
 
         half = T // 2
         y_bf = [sb.tile([P, half, LANES], BF16, name="y_bf%d" % h, align_bytes=64) for h in range(2)]
-        y_scales = sb.tile([P, half], U8, name="y_scales", align_bytes=64)
+        y_scales = sb.tile([P, T // LANES], U8, name="y_scales", align_bytes=64)
         y_codes = [sb.tile([P, w], U32, name="y_codes%d" % s, align_bytes=64) for s, w in enumerate(STORES)]
         stored = [slice(sum(STORES[:s]), sum(STORES[:s + 1])) for s in range(len(STORES))]
         last = LANES - 1
@@ -168,9 +168,9 @@ def tile_attend_gtucker_pl_kernel(tc, bT, cT, er, C, aoffs, boffs, coffs, out_0,
             nc.vector.tensor_copy(window[t][:].indirect(a_list[:]), da[t][:])
             nc.sync.dma_start(out_rows[:, t, :], window[t][:])
             if t < last - 1:
-                nc.gpsimd.tensor_scalar(y_bf[0][:, 0:DIRECT, t], window[t][:, 0:DIRECT], 1.0, -0.0, MULT, ADD)
+                nc.gpsimd.tensor_copy(y_bf[0][:, 0:DIRECT, t], window[t][:, 0:DIRECT])
             if t == last - 1:
-                nc.gpsimd.tensor_scalar(y_bf[0][:, 0:DIRECT, t:t + 2], window[t][:, 0:DIRECT].unsqueeze(2).to_broadcast([P, DIRECT, 2]), 1.0, -0.0, MULT, ADD)
+                nc.gpsimd.tensor_copy(y_bf[0][:, 0:DIRECT, t:t + 2], window[t][:, 0:DIRECT].unsqueeze(2).to_broadcast([P, DIRECT, 2]))
             nc.scalar.copy(pairs[:, t // 2, :, t % 2], window[t][:, DIRECT:high])
             if t < last:
                 nc.scalar.copy(y_bf[1][:, high - half:half, t], window[t][:, high:T])
@@ -190,15 +190,16 @@ def tile_attend_gtucker_pl_kernel(tc, bT, cT, er, C, aoffs, boffs, coffs, out_0,
         for run in cols:
             h, first = divmod(run.start, half)
             width = run.stop - run.start
+            plane, byte = divmod(run.start, T // LANES)
             s = [k for k in range(len(STORES)) if stored[k].start <= run.start][-1]
             word = run.start - stored[s].start
             nc.vector.quantize_mx(
                 out=y_codes[s][:, word:word + width].bitcast(E4M3),
-                scales=y_scales[LANES * h:P, first:first + width],
+                scales=y_scales[LANES * plane:P, byte:byte + width],
                 in_=y_bf[h][:, first:first + width, :].rearrange("p c t -> p (c t)"),
             )
             if run.stop == stored[s].stop:
                 nc.sync.dma_start(out_words[:, stored[s]], y_codes[s][:].bitcast(I32))
         for quad in range(4):
             queue = nc.scalar if quad % 2 == 0 else nc.sync
-            queue.dma_start(out_scales[4 * quad:4 * quad + 4, :].rearrange("r (h x) -> h r x", h=2), y_scales[32 * quad:32 * quad + 8, :].bitcast(I32))
+            queue.dma_start(out_scales[4 * quad:4 * quad + 4, :].rearrange("r (h x) -> h r x", h=LANES), y_scales[32 * quad:32 * quad + 16, :].bitcast(I32))

@@ -19,13 +19,11 @@ D = 512
 N = 512
 T = 2048
 U = 1024
-STORES = (768, 768, 512)
+STORES = (1024, 512, 512)
 CORE_PIECES = ((0, 0, 512), (1, 0, 256), (1, 256, 512))
-WIDTHS = (256,) * 8
-DIRECT = 768
-PAIRED = T - 2 * DIRECT
-VECTOR_RUNS = (512, 256)
-SCALAR_RUNS = (512, 256)
+GROUPS = (256, 512, 512, 768)
+RUN = 256
+COPY = mybir.ActivationFunctionType.Copy
 
 FLOPS = 2 * F * D * N
 
@@ -130,75 +128,103 @@ def tile_attend_gtucker_pl_kernel(tc, bT, cT, er, C, aoffs, boffs, coffs, out_0,
             deal_core(h)
         for run in halves:
             nc.vector.tensor_copy(q_bf[:, run, 2:4], q_pair[1][:, :, run].rearrange("p e i -> p i e"))
-        for r, run in enumerate(halves):
+        def quantise_q(run):
             nc.vector.quantize_mx(out=q_codes[:, run].bitcast(E5M2), scales=q_scales[:, run], in_=q_bf[:, run, :].rearrange("p i t -> p (i t)"))
-            if r == 0:
-                quantise_core(0)
-        for t in range(1, LANES):
-            quantise_core(t)
 
-        da = []
-        for t in range(LANES):
-            acc = psum.tile([P, N], F32, name="acc%d" % t, tag="acc%d" % t)
+        quantise_q(halves[0])
+        quantise_core(1)
+        quantise_core(0)
+        quantise_q(halves[1])
+        quantise_core(2)
+        quantise_core(3)
+
+        def product(t, run):
+            acc = psum.tile([P, run.stop - run.start], F32, name="acc%d_%d" % (t, run.start))
             nc.tensor.matmul_mx(
                 out=acc[:],
                 lhsT=core_codes[:, t, :].bitcast(E4M3),
                 lhsT_scale=core_scales[:, t, :],
-                rhs=q_codes[:].bitcast(E5M2),
-                rhs_scale=q_scales[:],
+                rhs=q_codes[:, run].bitcast(E5M2),
+                rhs_scale=q_scales[:, run],
                 start=True,
                 stop=True,
             )
-            da_t = sb.tile([P, N], F32, name="da%d" % t)
-            if t == 0:
-                nc.vector.tensor_copy(da_t[:], acc[:])
-            else:
-                nc.scalar.copy(da_t[:], acc[:])
-            da.append(da_t)
+            return acc
 
-        half = T // 2
-        y_bf = [sb.tile([P, half, LANES], BF16, name="y_bf%d" % h, align_bytes=64) for h in range(2)]
+        whole = slice(0, N)
+        acc10 = product(1, halves[0])
+        acc00 = product(0, halves[0])
+        acc11 = product(1, halves[1])
+        acc01 = product(0, halves[1])
+        acc2 = product(2, whole)
+        acc30 = product(3, halves[0])
+        acc31 = product(3, halves[1])
+
+        da = [sb.tile([P, N], F32, name="da%d" % t) for t in range(LANES)]
+        groups = [slice(sum(GROUPS[:k]), sum(GROUPS[:k + 1])) for k in range(len(GROUPS))]
+        planar = [sb.tile([P, LANES, w], BF16, name="planar%d" % k, align_bytes=64) for k, w in enumerate(GROUPS)]
+        y_bf = [sb.tile([P, RUN, LANES], BF16, name="y_bf%d" % u, align_bytes=64) for u in range(T // RUN)]
         y_scales = sb.tile([P, T // LANES], U8, name="y_scales", align_bytes=64)
         y_codes = [sb.tile([P, w], U32, name="y_codes%d" % s, align_bytes=64) for s, w in enumerate(STORES)]
         stored = [slice(sum(STORES[:s]), sum(STORES[:s + 1])) for s in range(len(STORES))]
-        last = LANES - 1
-        pairs = sb.tile([P, 2, PAIRED, 2], BF16, name="pairs", align_bytes=64)
-        high = DIRECT + PAIRED
-        for t in range(LANES):
-            nc.vector.tensor_copy(window[t][:].indirect(a_list[:]), da[t][:])
-            nc.sync.dma_start(out_rows[:, t, :], window[t][:])
-            if t < last - 1:
-                nc.gpsimd.tensor_copy(y_bf[0][:, 0:DIRECT, t], window[t][:, 0:DIRECT])
-            if t == last - 1:
-                nc.gpsimd.tensor_copy(y_bf[0][:, 0:DIRECT, t:t + 2], window[t][:, 0:DIRECT].unsqueeze(2).to_broadcast([P, DIRECT, 2]))
-            nc.scalar.copy(pairs[:, t // 2, :, t % 2], window[t][:, DIRECT:high])
-            if t < last:
-                nc.scalar.copy(y_bf[1][:, high - half:half, t], window[t][:, high:T])
 
-        first = 0
-        for width in VECTOR_RUNS:
-            nc.vector.tensor_copy(y_bf[0][:, first:first + width, last], window[last][:, first:first + width])
-            first = first + width
-        first = high
-        for width in SCALAR_RUNS:
-            nc.scalar.copy(y_bf[1][:, first - half:first - half + width, last], window[last][:, first:first + width])
-            first = first + width
-        woven = pairs[:].rearrange("p h c e -> p c h e")
-        nc.vector.tensor_copy(y_bf[0][:, DIRECT:half, :].rearrange("p c (h e) -> p c h e", h=2), woven[:, 0:half - DIRECT])
-        nc.vector.tensor_copy(y_bf[1][:, 0:high - half, :].rearrange("p c (h e) -> p c h e", h=2), woven[:, half - DIRECT:PAIRED])
-        cols = [slice(sum(WIDTHS[:j]), sum(WIDTHS[:j + 1])) for j in range(len(WIDTHS))]
-        for run in cols:
-            h, first = divmod(run.start, half)
-            width = run.stop - run.start
-            plane, byte = divmod(run.start, T // LANES)
-            s = [k for k in range(len(STORES)) if stored[k].start <= run.start][-1]
-            word = run.start - stored[s].start
-            nc.vector.quantize_mx(
-                out=y_codes[s][:, word:word + width].bitcast(E4M3),
-                scales=y_scales[LANES * plane:P, byte:byte + width],
-                in_=y_bf[h][:, first:first + width, :].rearrange("p c t -> p (c t)"),
+        def scalar_scatter(t, run):
+            nc.scalar.activation(window[t][:].indirect(a_list[:, run.start // 16:run.stop // 16]), da[t][:, run], COPY)
+
+        def store(t):
+            nc.sync.dma_start(out_rows[:, t, :], window[t][:])
+
+        def round_lane(copy, t, k):
+            copy(planar[k][:, t, :], window[t][:, groups[k]])
+
+        nc.scalar.copy(da[1][:, halves[0]], acc10[:])
+        nc.vector.tensor_copy(da[0][:, halves[0]], acc00[:])
+        nc.scalar.copy(da[1][:, halves[1]], acc11[:])
+        nc.vector.tensor_copy(da[0][:, halves[1]], acc01[:])
+        nc.vector.tensor_copy(window[0][:].indirect(a_list[:]), da[0][:])
+        store(0)
+        scalar_scatter(1, halves[0])
+        nc.scalar.copy(da[2][:], acc2[:])
+        nc.scalar.copy(da[3][:, halves[0]], acc30[:])
+        scalar_scatter(1, halves[1])
+        store(1)
+        nc.vector.tensor_copy(window[2][:].indirect(a_list[:]), da[2][:])
+        store(2)
+        nc.scalar.copy(da[3][:, halves[1]], acc31[:])
+        scalar_scatter(3, halves[0])
+        scalar_scatter(3, halves[1])
+        store(3)
+
+        last = len(GROUPS) - 1
+        for k in range(len(GROUPS)):
+            round_lane(nc.gpsimd.tensor_copy, 0, k)
+        for k in range(last):
+            round_lane(nc.gpsimd.tensor_copy, 1, k)
+        for k in range(len(GROUPS)):
+            round_lane(nc.vector.tensor_copy, 2, k)
+        round_lane(nc.vector.tensor_copy, 1, last)
+        round_lane(nc.vector.tensor_copy, 3, 0)
+        for k in range(1, len(GROUPS)):
+            round_lane(nc.scalar.copy, 3, k)
+
+        for u in range(T // RUN):
+            start = u * RUN
+            k = [j for j in range(len(GROUPS)) if groups[j].start <= start][-1]
+            first = start - groups[k].start
+            copy = nc.scalar.copy if k == last else nc.vector.tensor_copy
+            copy(
+                y_bf[u][:].rearrange("p (c i) t -> p c t i", i=4),
+                planar[k][:, :, first:first + RUN].rearrange("p t (c i) -> p c t i", i=4),
             )
-            if run.stop == stored[s].stop:
+            plane, byte = divmod(start, T // LANES)
+            s = [j for j in range(len(STORES)) if stored[j].start <= start][-1]
+            word = start - stored[s].start
+            nc.vector.quantize_mx(
+                out=y_codes[s][:, word:word + RUN].bitcast(E4M3),
+                scales=y_scales[LANES * plane:P, byte:byte + RUN],
+                in_=y_bf[u][:].rearrange("p c t -> p (c t)"),
+            )
+            if start + RUN == stored[s].stop:
                 nc.sync.dma_start(out_words[:, stored[s]], y_codes[s][:].bitcast(I32))
         for quad in range(4):
             queue = nc.scalar if quad % 2 == 0 else nc.sync

@@ -1,6 +1,7 @@
 from contextlib import ExitStack
 
 import concourse.mybir as mybir
+from concourse.masks import make_identity
 
 F32 = mybir.dt.float32
 BF16 = mybir.dt.bfloat16
@@ -11,6 +12,7 @@ U8 = mybir.dt.uint8
 E4M3 = mybir.dt.float8_e4m3fn_x4
 E5M2 = mybir.dt.float8_e5m2_x4
 MULT = mybir.AluOpType.mult
+COPY = mybir.ActivationFunctionType.Copy
 
 P = 128
 LANES = 4
@@ -20,10 +22,8 @@ N = 512
 T = 2048
 U = 1024
 STORES = (1024, 512, 512)
-CORE_PIECES = ((0, 0, 512), (1, 0, 256), (1, 256, 512))
-GROUPS = (256, 512, 512, 768)
+GROUPS = (256, 768, 1024)
 RUN = 256
-COPY = mybir.ActivationFunctionType.Copy
 
 FLOPS = 2 * F * D * N
 
@@ -46,10 +46,15 @@ def tile_attend_gtucker_pl_kernel(tc, bT, cT, er, C, aoffs, boffs, coffs, out_0,
         out_words = out_1[0].rearrange("p c l -> p (c l)").bitcast(I32)
         out_scales = out_2[0].bitcast(I32)
 
+        hn = N // 2
+        hd = D // 2
+        halves = [slice(0, hn), slice(hn, N)]
+        whole = slice(0, N)
+
         b_tab = [sb.tile([P, U], F32, name="b_tab%d" % t) for t in range(LANES)]
         c_tab = [sb.tile([P, U], F32, name="c_tab%d" % t) for t in range(LANES)]
-        er_sb = sb.tile([P, N], F32, name="er_sb")
-        core = [sb.tile([P, 2, stop - start], F32, name="core%d" % h) for h, (pair, start, stop) in enumerate(CORE_PIECES)]
+        er_col = sb.tile([P, LANES], F32, name="er_col")
+        core = [sb.tile([P, LANES, hd], F32, name="core%d" % h) for h in range(2)]
 
         def load_b(t):
             nc.sync.dma_start(b_tab[t][:], b_rows[:, t, :])
@@ -57,86 +62,111 @@ def tile_attend_gtucker_pl_kernel(tc, bT, cT, er, C, aoffs, boffs, coffs, out_0,
         def load_c(t):
             nc.sync.dma_start(c_tab[t][:], c_rows[:, t, :])
 
-        def load_core(h):
-            pair, start, stop = CORE_PIECES[h]
-            nc.sync.dma_start(core[h][:], core_rows[:, 2 * pair:2 * pair + 2, start:stop])
-
-        nc.sync.dma_start(b_list[:], boffs)
-        nc.sync.dma_start(er_sb[:], er)
+        nc.sync.dma_start(er_col[:], er[0].rearrange("(p m) -> p m", m=LANES))
         load_b(0)
+        nc.sync.dma_start(b_list[:], boffs)
         load_b(1)
+        load_b(2)
         nc.sync.dma_start(c_list[:], coffs)
         load_c(0)
-        load_c(1)
-        load_b(2)
         load_b(3)
-        load_core(0)
+        load_c(1)
         load_c(2)
         load_c(3)
-        load_core(1)
-        load_core(2)
+        for h in range(2):
+            nc.sync.dma_start(core[h][:], core_rows[:, :, h * hd:(h + 1) * hd])
         nc.sync.dma_start(a_list[:], aoffs)
+
+        identity = sb.tile([P, P], F32, name="identity")
+        make_identity(nc, identity[:])
+        er_wide = sb.tile([P, LANES, P], F32, name="er_wide")
+        nc.scalar.copy(er_wide[:], er_col[:].unsqueeze(2).to_broadcast([P, LANES, P]))
+        er_bank = psum.tile([P, LANES, P], F32, name="er_bank")
+        for m in range(LANES):
+            nc.tensor.transpose(er_bank[:, m, :], er_wide[:, m, :], identity[:])
 
         window = [sb.tile([P, T], F32, name="window%d" % t) for t in range(LANES)]
         for t in range(LANES):
             nc.gpsimd.memset(window[t][:].bitcast(I32), 0)
 
-        q_bf = sb.tile([P, N, LANES], BF16, name="q_bf", align_bytes=64)
-        q_pair = [sb.tile([P, 2, N], F32, name="q_pair%d" % h, tag="q_pair%d" % h, align_bytes=64) for h in range(2)]
-        eb = [sb.tile([P, N], F32, name="eb%d" % t, tag="eb%d" % t, align_bytes=64) for t in range(LANES)]
-
-        def gather_b(t):
-            nc.vector.tensor_tensor(eb[t][:], b_tab[t][:].indirect(b_list[:]), er_sb[:], MULT)
-
-        def gather_c(t, run):
-            h, e = divmod(t, 2)
-            nc.vector.tensor_tensor(q_pair[h][:, e, run], c_tab[t][:].indirect(c_list[:, run.start // 16:run.stop // 16]), eb[t][:, run], MULT)
-
-        core_codes = sb.tile([P, LANES, P], U32, name="core_codes", align_bytes=64)
-        core_scales = sb.tile([P, LANES, P], U8, name="core_scales", align_bytes=64)
+        gb = [sb.tile([P, N], F32, name="gb%d" % t) for t in range(LANES)]
+        eb = [sb.tile([P, N], F32, name="eb%d" % t) for t in range(LANES)]
+        q = sb.tile([P, LANES, N], F32, name="q")
+        q_bf = [sb.tile([P, hn, LANES], BF16, name="q_bf%d" % h, align_bytes=64) for h in range(2)]
         q_codes = sb.tile([P, N], U32, name="q_codes", align_bytes=64)
         q_scales = sb.tile([P, N], U8, name="q_scales", align_bytes=64)
+        core_bf = [sb.tile([P, 2, P, LANES], BF16, name="core_bf%d" % g, align_bytes=64) for g in range(2)]
+        core_codes = sb.tile([P, LANES, P], U32, name="core_codes", align_bytes=64)
+        core_scales = sb.tile([P, LANES, P], U8, name="core_scales", align_bytes=64)
 
-        def deal_core(h):
-            pair, start, stop = CORE_PIECES[h]
+        def gather_b(t):
+            nc.scalar.activation(gb[t][:], b_tab[t][:].indirect(b_list[:]), COPY)
+
+        def times_er(t):
+            nc.vector.tensor_tensor(
+                eb[t][:].rearrange("p (n m) -> p n m", m=LANES),
+                gb[t][:].rearrange("p (n m) -> p n m", m=LANES),
+                er_bank[:].rearrange("p m n -> p n m"),
+                MULT,
+            )
+
+        def offsets(index, run):
+            return index[:, run.start // 16:run.stop // 16]
+
+        def gather_c(t, run):
+            nc.vector.tensor_tensor(q[:, t, run], c_tab[t][:].indirect(offsets(c_list, run)), eb[t][:, run], MULT)
+
+        def gather_c_plain(t, run):
+            gc = sb.tile([P, run.stop - run.start], F32, name="gc%d" % t)
+            nc.scalar.activation(gc[:], c_tab[t][:].indirect(offsets(c_list, run)), COPY)
+            return gc
+
+        def round_q(h):
+            nc.vector.tensor_copy(
+                q_bf[h][:].rearrange("p (c i) t -> p c t i", i=4),
+                q[:, :, halves[h]].rearrange("p t (c i) -> p c t i", i=4),
+            )
+
+        def quantise_q(h):
+            nc.vector.quantize_mx(out=q_codes[:, halves[h]].bitcast(E5M2), scales=q_scales[:, halves[h]], in_=q_bf[h][:].rearrange("p i t -> p (i t)"))
+
+        def deal_core(h, g):
             nc.scalar.copy(
-                core_bf[:, :, start // LANES:stop // LANES, 2 * pair:2 * pair + 2].rearrange("p t m j -> p m j t"),
-                core[h][:].rearrange("p j (m t) -> p m j t", t=LANES),
+                core_bf[g][:, :, h * hd // LANES:(h + 1) * hd // LANES, :].rearrange("p e m j -> p m e j"),
+                core[h][:].rearrange("p j (m t) -> p m t j", t=LANES)[:, :, 2 * g:2 * g + 2, :],
             )
 
         def quantise_core(t):
             nc.vector.quantize_mx(
                 out=core_codes[:, t, :].bitcast(E4M3),
                 scales=core_scales[:, t, :],
-                in_=core_bf[:, t, :, :].rearrange("p m j -> p (m j)"),
+                in_=core_bf[t // 2][:, t % 2, :, :].rearrange("p m j -> p (m j)"),
             )
 
-        hn = N // 2
-        halves = [slice(0, hn), slice(hn, N)]
-        gather_b(0)
-        gather_b(1)
-        gather_c(0, slice(0, N))
-        gather_c(1, slice(0, N))
-        nc.scalar.copy(q_bf[:, :, 0:2], q_pair[0][:].rearrange("p e i -> p i e"))
-        gather_b(2)
-        gather_b(3)
-        gather_c(2, slice(0, N))
-        for run in halves:
-            gather_c(3, run)
-        core_bf = sb.tile([P, LANES, P, LANES], BF16, name="core_bf", tag="q_pair0", align_bytes=64)
-        for h in range(len(CORE_PIECES)):
-            deal_core(h)
-        for run in halves:
-            nc.vector.tensor_copy(q_bf[:, run, 2:4], q_pair[1][:, :, run].rearrange("p e i -> p i e"))
-        def quantise_q(run):
-            nc.vector.quantize_mx(out=q_codes[:, run].bitcast(E5M2), scales=q_scales[:, run], in_=q_bf[:, run, :].rearrange("p i t -> p (i t)"))
-
-        quantise_q(halves[0])
-        quantise_core(1)
+        for t in range(LANES):
+            gather_b(t)
+        times_er(0)
+        times_er(1)
+        gather_c(0, whole)
+        times_er(2)
+        gather_c(1, whole)
+        times_er(3)
+        gc2 = gather_c_plain(2, whole)
+        gather_c(3, halves[0])
+        gc3 = gather_c_plain(3, halves[1])
+        nc.vector.tensor_tensor(q[:, 2, :], gc2[:], eb[2][:], MULT)
+        nc.vector.tensor_tensor(q[:, 3, halves[1]], gc3[:], eb[3][:, halves[1]], MULT)
+        for h in range(2):
+            for g in range(2):
+                deal_core(h, g)
+        for h in range(2):
+            round_q(h)
+        quantise_q(0)
         quantise_core(0)
-        quantise_q(halves[1])
-        quantise_core(2)
+        quantise_q(1)
+        quantise_core(1)
         quantise_core(3)
+        quantise_core(2)
 
         def product(t, run):
             acc = psum.tile([P, run.stop - run.start], F32, name="acc%d_%d" % (t, run.start))
@@ -151,14 +181,13 @@ def tile_attend_gtucker_pl_kernel(tc, bT, cT, er, C, aoffs, boffs, coffs, out_0,
             )
             return acc
 
-        whole = slice(0, N)
-        acc10 = product(1, halves[0])
         acc00 = product(0, halves[0])
-        acc11 = product(1, halves[1])
         acc01 = product(0, halves[1])
-        acc2 = product(2, whole)
+        acc10 = product(1, halves[0])
+        acc11 = product(1, halves[1])
         acc30 = product(3, halves[0])
         acc31 = product(3, halves[1])
+        acc2 = product(2, whole)
 
         da = [sb.tile([P, N], F32, name="da%d" % t) for t in range(LANES)]
         groups = [slice(sum(GROUPS[:k]), sum(GROUPS[:k + 1])) for k in range(len(GROUPS))]
@@ -177,17 +206,17 @@ def tile_attend_gtucker_pl_kernel(tc, bT, cT, er, C, aoffs, boffs, coffs, out_0,
         def round_lane(copy, t, k):
             copy(planar[k][:, t, :], window[t][:, groups[k]])
 
+        nc.scalar.copy(da[0][:, halves[0]], acc00[:])
+        nc.scalar.copy(da[0][:, halves[1]], acc01[:])
         nc.scalar.copy(da[1][:, halves[0]], acc10[:])
-        nc.vector.tensor_copy(da[0][:, halves[0]], acc00[:])
         nc.scalar.copy(da[1][:, halves[1]], acc11[:])
-        nc.vector.tensor_copy(da[0][:, halves[1]], acc01[:])
         nc.vector.tensor_copy(window[0][:].indirect(a_list[:]), da[0][:])
         store(0)
         scalar_scatter(1, halves[0])
-        nc.scalar.copy(da[2][:], acc2[:])
         nc.scalar.copy(da[3][:, halves[0]], acc30[:])
         scalar_scatter(1, halves[1])
         store(1)
+        nc.vector.tensor_copy(da[2][:], acc2[:])
         nc.vector.tensor_copy(window[2][:].indirect(a_list[:]), da[2][:])
         store(2)
         nc.scalar.copy(da[3][:, halves[1]], acc31[:])
@@ -198,14 +227,14 @@ def tile_attend_gtucker_pl_kernel(tc, bT, cT, er, C, aoffs, boffs, coffs, out_0,
         last = len(GROUPS) - 1
         for k in range(len(GROUPS)):
             round_lane(nc.gpsimd.tensor_copy, 0, k)
-        for k in range(last):
-            round_lane(nc.gpsimd.tensor_copy, 1, k)
+        round_lane(nc.gpsimd.tensor_copy, 1, 0)
         for k in range(len(GROUPS)):
             round_lane(nc.vector.tensor_copy, 2, k)
         round_lane(nc.vector.tensor_copy, 1, last)
-        round_lane(nc.vector.tensor_copy, 3, 0)
-        for k in range(1, len(GROUPS)):
-            round_lane(nc.scalar.copy, 3, k)
+        round_lane(nc.vector.tensor_copy, 1, 1)
+        for k in range(last):
+            round_lane(nc.vector.tensor_copy, 3, k)
+        round_lane(nc.scalar.copy, 3, last)
 
         for u in range(T // RUN):
             start = u * RUN

@@ -21,8 +21,8 @@ D = 512
 N = 512
 T = 2048
 U = 1024
-STORES = (1024, 512, 512)
-GROUPS = (256, 768, 1024)
+STORES = (768, 768, 512)
+GROUPS = (256, 1024, 512, 256)
 RUN = 256
 
 FLOPS = 2 * F * D * N
@@ -91,7 +91,7 @@ def tile_attend_gtucker_pl_kernel(tc, bT, cT, er, C, aoffs, boffs, coffs, out_0,
 
         gb = [sb.tile([P, N], F32, name="gb%d" % t) for t in range(LANES)]
         eb = [sb.tile([P, N], F32, name="eb%d" % t) for t in range(LANES)]
-        q = sb.tile([P, LANES, N], F32, name="q")
+        q = [sb.tile([P, LANES, hn], F32, name="q%d" % h) for h in range(2)]
         q_bf = [sb.tile([P, hn, LANES], BF16, name="q_bf%d" % h, align_bytes=64) for h in range(2)]
         q_codes = sb.tile([P, N], U32, name="q_codes", align_bytes=64)
         q_scales = sb.tile([P, N], U8, name="q_scales", align_bytes=64)
@@ -113,8 +113,8 @@ def tile_attend_gtucker_pl_kernel(tc, bT, cT, er, C, aoffs, boffs, coffs, out_0,
         def offsets(index, run):
             return index[:, run.start // 16:run.stop // 16]
 
-        def gather_c(t, run):
-            nc.vector.tensor_tensor(q[:, t, run], c_tab[t][:].indirect(offsets(c_list, run)), eb[t][:, run], MULT)
+        def gather_c(t, h):
+            nc.vector.tensor_tensor(q[h][:, t, :], c_tab[t][:].indirect(offsets(c_list, halves[h])), eb[t][:, halves[h]], MULT)
 
         def gather_c_plain(t, run):
             gc = sb.tile([P, run.stop - run.start], F32, name="gc%d" % t)
@@ -124,7 +124,7 @@ def tile_attend_gtucker_pl_kernel(tc, bT, cT, er, C, aoffs, boffs, coffs, out_0,
         def round_q(h):
             nc.vector.tensor_copy(
                 q_bf[h][:].rearrange("p (c i) t -> p c t i", i=4),
-                q[:, :, halves[h]].rearrange("p t (c i) -> p c t i", i=4),
+                q[h][:].rearrange("p t (c i) -> p c t i", i=4),
             )
 
         def quantise_q(h):
@@ -147,26 +147,27 @@ def tile_attend_gtucker_pl_kernel(tc, bT, cT, er, C, aoffs, boffs, coffs, out_0,
             gather_b(t)
         times_er(0)
         times_er(1)
-        gather_c(0, whole)
+        gather_c(0, 0)
+        gather_c(0, 1)
         times_er(2)
-        gather_c(1, whole)
+        gather_c(1, 0)
+        gather_c(1, 1)
         times_er(3)
         gc2 = gather_c_plain(2, whole)
-        gather_c(3, halves[0])
+        gather_c(3, 0)
         gc3 = gather_c_plain(3, halves[1])
-        nc.vector.tensor_tensor(q[:, 2, :], gc2[:], eb[2][:], MULT)
-        nc.vector.tensor_tensor(q[:, 3, halves[1]], gc3[:], eb[3][:, halves[1]], MULT)
+        for h in range(2):
+            nc.vector.tensor_tensor(q[h][:, 2, :], gc2[:, halves[h]], eb[2][:, halves[h]], MULT)
+        round_q(0)
+        nc.vector.tensor_tensor(q[1][:, 3, :], gc3[:], eb[3][:, halves[1]], MULT)
+        quantise_q(0)
+        round_q(1)
         for h in range(2):
             for g in range(2):
                 deal_core(h, g)
-        for h in range(2):
-            round_q(h)
-        quantise_q(0)
         quantise_core(0)
         quantise_q(1)
         quantise_core(1)
-        quantise_core(3)
-        quantise_core(2)
 
         def product(t, run):
             acc = psum.tile([P, run.stop - run.start], F32, name="acc%d_%d" % (t, run.start))
@@ -185,9 +186,6 @@ def tile_attend_gtucker_pl_kernel(tc, bT, cT, er, C, aoffs, boffs, coffs, out_0,
         acc01 = product(0, halves[1])
         acc10 = product(1, halves[0])
         acc11 = product(1, halves[1])
-        acc30 = product(3, halves[0])
-        acc31 = product(3, halves[1])
-        acc2 = product(2, whole)
 
         da = [sb.tile([P, N], F32, name="da%d" % t) for t in range(LANES)]
         groups = [slice(sum(GROUPS[:k]), sum(GROUPS[:k + 1])) for k in range(len(GROUPS))]
@@ -210,37 +208,43 @@ def tile_attend_gtucker_pl_kernel(tc, bT, cT, er, C, aoffs, boffs, coffs, out_0,
         nc.scalar.copy(da[0][:, halves[1]], acc01[:])
         nc.scalar.copy(da[1][:, halves[0]], acc10[:])
         nc.scalar.copy(da[1][:, halves[1]], acc11[:])
-        nc.vector.tensor_copy(window[0][:].indirect(a_list[:]), da[0][:])
+        nc.vector.tensor_copy(window[0][:].indirect(offsets(a_list, halves[0])), da[0][:, halves[0]])
+        quantise_core(3)
+        quantise_core(2)
+        acc30 = product(3, halves[0])
+        acc2 = product(2, whole)
+        acc31 = product(3, halves[1])
+        nc.vector.tensor_copy(window[0][:].indirect(offsets(a_list, halves[1])), da[0][:, halves[1]])
         store(0)
         scalar_scatter(1, halves[0])
         nc.scalar.copy(da[3][:, halves[0]], acc30[:])
+        nc.scalar.copy(da[2][:], acc2[:])
+        nc.scalar.copy(da[3][:, halves[1]], acc31[:])
+        nc.vector.tensor_copy(window[3][:].indirect(offsets(a_list, halves[0])), da[3][:, halves[0]])
         scalar_scatter(1, halves[1])
         store(1)
-        nc.vector.tensor_copy(da[2][:], acc2[:])
-        nc.vector.tensor_copy(window[2][:].indirect(a_list[:]), da[2][:])
-        store(2)
-        nc.scalar.copy(da[3][:, halves[1]], acc31[:])
-        scalar_scatter(3, halves[0])
         scalar_scatter(3, halves[1])
         store(3)
+        nc.vector.tensor_copy(window[2][:].indirect(a_list[:]), da[2][:])
+        store(2)
 
         last = len(GROUPS) - 1
         for k in range(len(GROUPS)):
             round_lane(nc.gpsimd.tensor_copy, 0, k)
-        round_lane(nc.gpsimd.tensor_copy, 1, 0)
-        for k in range(len(GROUPS)):
-            round_lane(nc.vector.tensor_copy, 2, k)
-        round_lane(nc.vector.tensor_copy, 1, last)
-        round_lane(nc.vector.tensor_copy, 1, 1)
         for k in range(last):
-            round_lane(nc.vector.tensor_copy, 3, k)
-        round_lane(nc.scalar.copy, 3, last)
+            round_lane(nc.gpsimd.tensor_copy, 1, k)
+        round_lane(nc.scalar.copy, 1, last)
+        for k in range(len(GROUPS)):
+            round_lane(nc.scalar.copy, 3, k)
+        for k in range(last):
+            round_lane(nc.vector.tensor_copy, 2, k)
+        round_lane(nc.scalar.copy, 2, last)
 
         for u in range(T // RUN):
             start = u * RUN
             k = [j for j in range(len(GROUPS)) if groups[j].start <= start][-1]
             first = start - groups[k].start
-            copy = nc.scalar.copy if k == last else nc.vector.tensor_copy
+            copy = nc.scalar.copy if k >= last - 1 else nc.vector.tensor_copy
             copy(
                 y_bf[u][:].rearrange("p (c i) t -> p c t i", i=4),
                 planar[k][:, :, first:first + RUN].rearrange("p t (c i) -> p c t i", i=4),

@@ -62,7 +62,7 @@ def tile_attend_gtucker_pl_kernel(tc, bT, cT, er, C, aoffs, boffs, coffs, out_0,
         def load_c(t):
             nc.sync.dma_start(c_tab[t][:], c_rows[:, t, :])
 
-        nc.sync.dma_start(er_col[:], er[0].rearrange("(p m) -> p m", m=LANES))
+        nc.scalar.dma_start(er_col[:], er[0].rearrange("(p m) -> p m", m=LANES))
         load_b(0)
         nc.sync.dma_start(b_list[:], boffs)
         load_b(1)
@@ -150,24 +150,28 @@ def tile_attend_gtucker_pl_kernel(tc, bT, cT, er, C, aoffs, boffs, coffs, out_0,
         gather_c(0, 0)
         gather_c(0, 1)
         times_er(2)
+        gc = {t: gather_c_plain(t, halves[1]) for t in range(1, LANES)}
+
+        def times_c(t):
+            nc.vector.tensor_tensor(q[1][:, t, :], gc[t][:], eb[t][:, halves[1]], MULT)
+
         gather_c(1, 0)
-        gather_c(1, 1)
         times_er(3)
-        gc2 = gather_c_plain(2, whole)
+        gather_c(2, 0)
+        times_c(1)
         gather_c(3, 0)
-        gc3 = gather_c_plain(3, halves[1])
+        times_c(2)
+        times_c(3)
         for h in range(2):
-            nc.vector.tensor_tensor(q[h][:, 2, :], gc2[:, halves[h]], eb[2][:, halves[h]], MULT)
-        round_q(0)
-        nc.vector.tensor_tensor(q[1][:, 3, :], gc3[:], eb[3][:, halves[1]], MULT)
-        quantise_q(0)
-        round_q(1)
+            round_q(h)
+        for h in range(2):
+            quantise_q(h)
         for h in range(2):
             for g in range(2):
                 deal_core(h, g)
         quantise_core(0)
-        quantise_q(1)
         quantise_core(1)
+        quantise_core(3)
 
         def product(t, run):
             acc = psum.tile([P, run.stop - run.start], F32, name="acc%d_%d" % (t, run.start))
@@ -209,7 +213,6 @@ def tile_attend_gtucker_pl_kernel(tc, bT, cT, er, C, aoffs, boffs, coffs, out_0,
         nc.scalar.copy(da[1][:, halves[0]], acc10[:])
         nc.scalar.copy(da[1][:, halves[1]], acc11[:])
         nc.vector.tensor_copy(window[0][:].indirect(offsets(a_list, halves[0])), da[0][:, halves[0]])
-        quantise_core(3)
         quantise_core(2)
         acc30 = product(3, halves[0])
         acc2 = product(2, whole)
@@ -236,9 +239,8 @@ def tile_attend_gtucker_pl_kernel(tc, bT, cT, er, C, aoffs, boffs, coffs, out_0,
         round_lane(nc.scalar.copy, 1, last)
         for k in range(len(GROUPS)):
             round_lane(nc.scalar.copy, 3, k)
-        for k in range(last):
-            round_lane(nc.vector.tensor_copy, 2, k)
-        round_lane(nc.scalar.copy, 2, last)
+        for k in range(len(GROUPS)):
+            round_lane(nc.scalar.copy if k >= last - 1 else nc.vector.tensor_copy, 2, k)
 
         for u in range(T // RUN):
             start = u * RUN

@@ -22,7 +22,7 @@ N = 512
 T = 2048
 U = 1024
 STORES = (768, 768, 512)
-GROUPS = (256, 1024, 512, 256)
+GROUPS = (512, 768, 768)
 RUN = 256
 
 FLOPS = 2 * F * D * N
@@ -132,8 +132,8 @@ def tile_attend_gtucker_pl_kernel(tc, bT, cT, er, C, aoffs, boffs, coffs, out_0,
 
         def deal_core(h, g):
             nc.scalar.copy(
-                core_bf[g][:, :, h * hd // LANES:(h + 1) * hd // LANES, :].rearrange("p e m j -> p m e j"),
-                core[h][:].rearrange("p j (m t) -> p m t j", t=LANES)[:, :, 2 * g:2 * g + 2, :],
+                core_bf[g][:, :, h * hd // LANES:(h + 1) * hd // LANES, :].rearrange("p e m j -> p m j e"),
+                core[h][:].rearrange("p j (m t) -> p m j t", t=LANES)[:, :, :, 2 * g:2 * g + 2],
             )
 
         def quantise_core(t):
@@ -240,13 +240,13 @@ def tile_attend_gtucker_pl_kernel(tc, bT, cT, er, C, aoffs, boffs, coffs, out_0,
         for k in range(len(GROUPS)):
             round_lane(nc.scalar.copy, 3, k)
         for k in range(len(GROUPS)):
-            round_lane(nc.scalar.copy if k >= last - 1 else nc.vector.tensor_copy, 2, k)
+            round_lane(nc.vector.tensor_copy, 2, k)
 
         for u in range(T // RUN):
             start = u * RUN
             k = [j for j in range(len(GROUPS)) if groups[j].start <= start][-1]
             first = start - groups[k].start
-            copy = nc.scalar.copy if k >= last - 1 else nc.vector.tensor_copy
+            copy = nc.scalar.copy if k == last else nc.vector.tensor_copy
             copy(
                 y_bf[u][:].rearrange("p (c i) t -> p c t i", i=4),
                 planar[k][:, :, first:first + RUN].rearrange("p t (c i) -> p c t i", i=4),

@@ -22,7 +22,8 @@ N = 512
 T = 2048
 U = 1024
 STORES = (768, 768, 512)
-GROUPS = (512, 768, 768)
+GROUPS = (1536, 512)
+SCALAR_RUNS = (1, 3, 5, 7)
 RUN = 256
 
 FLOPS = 2 * F * D * N
@@ -242,15 +243,20 @@ def tile_attend_gtucker_pl_kernel(tc, bT, cT, er, C, aoffs, boffs, coffs, out_0,
         for k in range(len(GROUPS)):
             round_lane(nc.vector.tensor_copy, 2, k)
 
-        for u in range(T // RUN):
-            start = u * RUN
-            k = [j for j in range(len(GROUPS)) if groups[j].start <= start][-1]
-            first = start - groups[k].start
-            copy = nc.scalar.copy if k == last else nc.vector.tensor_copy
+        def weave(copy, u, first, width):
+            k = [j for j in range(len(GROUPS)) if groups[j].start <= u * RUN][-1]
+            column = u * RUN - groups[k].start + first
             copy(
-                y_bf[u][:].rearrange("p (c i) t -> p c t i", i=4),
-                planar[k][:, :, first:first + RUN].rearrange("p t (c i) -> p c t i", i=4),
+                y_bf[u][:, first:first + width, :].rearrange("p (c i) t -> p c t i", i=4),
+                planar[k][:, :, column:column + width].rearrange("p t (c i) -> p c t i", i=4),
             )
+
+        for u in range(T // RUN):
+            if u in SCALAR_RUNS:
+                weave(nc.scalar.copy, u, 0, RUN)
+            else:
+                weave(nc.vector.tensor_copy, u, 0, RUN)
+            start = u * RUN
             plane, byte = divmod(start, T // LANES)
             s = [j for j in range(len(STORES)) if stored[j].start <= start][-1]
             word = start - stored[s].start

@@ -25,6 +25,7 @@ STORES = (768, 768, 512)
 GROUPS = (1536, 512)
 SCALAR_RUNS = (1, 3, 5, 7)
 RUN = 256
+VECTOR_ENTRIES = 128
 
 FLOPS = 2 * F * D * N
 
@@ -34,6 +35,7 @@ def tile_attend_gtucker_pl_kernel(tc, bT, cT, er, C, aoffs, boffs, coffs, out_0,
     with ExitStack() as ctx:
         lists = ctx.enter_context(tc.tile_pool(name="lists", bufs=1))
         sb = ctx.enter_context(tc.tile_pool(name="sb", bufs=1))
+        shared = ctx.enter_context(tc.tile_pool(name="shared", bufs=1))
         psum = ctx.enter_context(tc.psum_pool(name="psum", bufs=1))
 
         a_list = lists.tile([P, N // 16], U16, name="a_list")
@@ -48,34 +50,23 @@ def tile_attend_gtucker_pl_kernel(tc, bT, cT, er, C, aoffs, boffs, coffs, out_0,
         out_scales = out_2[0].bitcast(I32)
 
         hn = N // 2
-        hd = D // 2
         halves = [slice(0, hn), slice(hn, N)]
         whole = slice(0, N)
 
         b_tab = [sb.tile([P, U], F32, name="b_tab%d" % t) for t in range(LANES)]
         c_tab = [sb.tile([P, U], F32, name="c_tab%d" % t) for t in range(LANES)]
         er_col = sb.tile([P, LANES], F32, name="er_col")
-        core = [sb.tile([P, LANES, hd], F32, name="core%d" % h) for h in range(2)]
+        core = sb.tile([P, LANES, D], F32, name="core")
 
-        def load_b(t):
-            nc.sync.dma_start(b_tab[t][:], b_rows[:, t, :])
-
-        def load_c(t):
-            nc.sync.dma_start(c_tab[t][:], c_rows[:, t, :])
-
-        nc.scalar.dma_start(er_col[:], er[0].rearrange("(p m) -> p m", m=LANES))
-        load_b(0)
+        nc.sync.dma_start(er_col[:], er[0].rearrange("(p m) -> p m", m=LANES))
+        nc.sync.dma_start(b_tab[0][:], b_rows[:, 0, :])
         nc.sync.dma_start(b_list[:], boffs)
-        load_b(1)
-        load_b(2)
+        for t in range(1, LANES):
+            nc.sync.dma_start(b_tab[t][:], b_rows[:, t, :])
         nc.sync.dma_start(c_list[:], coffs)
-        load_c(0)
-        load_b(3)
-        load_c(1)
-        load_c(2)
-        load_c(3)
-        for h in range(2):
-            nc.sync.dma_start(core[h][:], core_rows[:, :, h * hd:(h + 1) * hd])
+        for t in range(LANES):
+            nc.sync.dma_start(c_tab[t][:], c_rows[:, t, :])
+        nc.sync.dma_start(core[:], core_rows)
         nc.sync.dma_start(a_list[:], aoffs)
 
         identity = sb.tile([P, P], F32, name="identity")
@@ -92,38 +83,42 @@ def tile_attend_gtucker_pl_kernel(tc, bT, cT, er, C, aoffs, boffs, coffs, out_0,
 
         gb = [sb.tile([P, N], F32, name="gb%d" % t) for t in range(LANES)]
         eb = [sb.tile([P, N], F32, name="eb%d" % t) for t in range(LANES)]
-        q = [sb.tile([P, LANES, hn], F32, name="q%d" % h) for h in range(2)]
+        gc = [sb.tile([P, N], F32, name="gc%d" % t) for t in range(LANES)]
+        q = [shared.tile([P, LANES, hn], F32, name="q%d" % h, offset=h * LANES * hn * 4, align_bytes=64) for h in range(2)]
         q_bf = [sb.tile([P, hn, LANES], BF16, name="q_bf%d" % h, align_bytes=64) for h in range(2)]
         q_codes = sb.tile([P, N], U32, name="q_codes", align_bytes=64)
         q_scales = sb.tile([P, N], U8, name="q_scales", align_bytes=64)
-        core_bf = [sb.tile([P, 2, P, LANES], BF16, name="core_bf%d" % g, align_bytes=64) for g in range(2)]
-        core_codes = sb.tile([P, LANES, P], U32, name="core_codes", align_bytes=64)
-        core_scales = sb.tile([P, LANES, P], U8, name="core_scales", align_bytes=64)
+        core_bf = [shared.tile([P, 2, P, LANES], BF16, name="core_bf%d" % g, offset=g * 2 * P * LANES * 2, align_bytes=64) for g in range(2)]
+        core_codes = [sb.tile([P, 2, P], U32, name="core_codes%d" % g, align_bytes=64) for g in range(2)]
+        core_scales = [sb.tile([P, 2, P], U8, name="core_scales%d" % g, align_bytes=64) for g in range(2)]
 
-        def gather_b(t):
-            nc.scalar.activation(gb[t][:], b_tab[t][:].indirect(b_list[:]), COPY)
+        def offsets(index, run):
+            return index[:, run.start // 16:run.stop // 16]
 
-        def times_er(t):
+        def split(first):
+            return slice(0, first), slice(first, N)
+
+        for t in range(LANES):
+            on_vector, on_scalar = split(VECTOR_ENTRIES)
+            nc.scalar.activation(gb[t][:, on_scalar], b_tab[t][:].indirect(offsets(b_list, on_scalar)), COPY)
+            nc.vector.tensor_copy(gb[t][:, on_vector], b_tab[t][:].indirect(offsets(b_list, on_vector)))
             nc.vector.tensor_tensor(
                 eb[t][:].rearrange("p (n m) -> p n m", m=LANES),
                 gb[t][:].rearrange("p (n m) -> p n m", m=LANES),
                 er_bank[:].rearrange("p m n -> p n m"),
                 MULT,
             )
+        for t in range(LANES):
+            on_vector, on_scalar = split(hn if t == LANES - 1 else VECTOR_ENTRIES)
+            nc.scalar.activation(gc[t][:, on_scalar], c_tab[t][:].indirect(offsets(c_list, on_scalar)), COPY)
+            nc.vector.tensor_tensor(q[0][:, t, on_vector], c_tab[t][:].indirect(offsets(c_list, on_vector)), eb[t][:, on_vector], MULT)
+            if on_scalar.start < hn:
+                rest = slice(on_scalar.start, hn)
+                nc.vector.tensor_tensor(q[0][:, t, rest], gc[t][:, rest], eb[t][:, rest], MULT)
+            nc.vector.tensor_tensor(q[1][:, t, :], gc[t][:, halves[1]], eb[t][:, halves[1]], MULT)
 
-        def offsets(index, run):
-            return index[:, run.start // 16:run.stop // 16]
-
-        def gather_c(t, h):
-            nc.vector.tensor_tensor(q[h][:, t, :], c_tab[t][:].indirect(offsets(c_list, halves[h])), eb[t][:, halves[h]], MULT)
-
-        def gather_c_plain(t, run):
-            gc = sb.tile([P, run.stop - run.start], F32, name="gc%d" % t)
-            nc.scalar.activation(gc[:], c_tab[t][:].indirect(offsets(c_list, run)), COPY)
-            return gc
-
-        def round_q(h):
-            nc.vector.tensor_copy(
+        def round_q(copy, h):
+            copy(
                 q_bf[h][:].rearrange("p (c i) t -> p c t i", i=4),
                 q[h][:].rearrange("p t (c i) -> p c t i", i=4),
             )
@@ -131,55 +126,35 @@ def tile_attend_gtucker_pl_kernel(tc, bT, cT, er, C, aoffs, boffs, coffs, out_0,
         def quantise_q(h):
             nc.vector.quantize_mx(out=q_codes[:, halves[h]].bitcast(E5M2), scales=q_scales[:, halves[h]], in_=q_bf[h][:].rearrange("p i t -> p (i t)"))
 
-        def deal_core(h, g):
-            nc.scalar.copy(
-                core_bf[g][:, :, h * hd // LANES:(h + 1) * hd // LANES, :].rearrange("p e m j -> p m j e"),
-                core[h][:].rearrange("p j (m t) -> p m j t", t=LANES)[:, :, :, 2 * g:2 * g + 2],
+        def deal_core(copy, g):
+            copy(
+                core_bf[g][:].rearrange("p e m j -> p m j e"),
+                core[:].rearrange("p j (m t) -> p m j t", t=LANES)[:, :, :, 2 * g:2 * g + 2],
             )
 
-        def quantise_core(t):
+        def quantise_core(g, first, last):
             nc.vector.quantize_mx(
-                out=core_codes[:, t, :].bitcast(E4M3),
-                scales=core_scales[:, t, :],
-                in_=core_bf[t // 2][:, t % 2, :, :].rearrange("p m j -> p (m j)"),
+                out=core_codes[g][:, first:last, :].rearrange("p e m -> p (e m)").bitcast(E4M3),
+                scales=core_scales[g][:, first:last, :].rearrange("p e m -> p (e m)"),
+                in_=core_bf[g][:, first:last, :, :].rearrange("p e m j -> p (e m j)"),
             )
 
-        for t in range(LANES):
-            gather_b(t)
-        times_er(0)
-        times_er(1)
-        gather_c(0, 0)
-        gather_c(0, 1)
-        times_er(2)
-        gc = {t: gather_c_plain(t, halves[1]) for t in range(1, LANES)}
-
-        def times_c(t):
-            nc.vector.tensor_tensor(q[1][:, t, :], gc[t][:], eb[t][:, halves[1]], MULT)
-
-        gather_c(1, 0)
-        times_er(3)
-        gather_c(2, 0)
-        times_c(1)
-        gather_c(3, 0)
-        times_c(2)
-        times_c(3)
-        for h in range(2):
-            round_q(h)
-        for h in range(2):
-            quantise_q(h)
-        for h in range(2):
-            for g in range(2):
-                deal_core(h, g)
-        quantise_core(0)
-        quantise_core(1)
-        quantise_core(3)
+        round_q(nc.vector.tensor_copy, 0)
+        round_q(nc.scalar.copy, 1)
+        deal_core(nc.vector.tensor_copy, 0)
+        quantise_q(0)
+        quantise_core(0, 0, 1)
+        quantise_q(1)
+        quantise_core(0, 1, 2)
+        deal_core(nc.scalar.copy, 1)
+        quantise_core(1, 0, 2)
 
         def product(t, run):
             acc = psum.tile([P, run.stop - run.start], F32, name="acc%d_%d" % (t, run.start))
             nc.tensor.matmul_mx(
                 out=acc[:],
-                lhsT=core_codes[:, t, :].bitcast(E4M3),
-                lhsT_scale=core_scales[:, t, :],
+                lhsT=core_codes[t // 2][:, t % 2, :].bitcast(E4M3),
+                lhsT_scale=core_scales[t // 2][:, t % 2, :],
                 rhs=q_codes[:, run].bitcast(E5M2),
                 rhs_scale=q_scales[:, run],
                 start=True,
@@ -213,12 +188,10 @@ def tile_attend_gtucker_pl_kernel(tc, bT, cT, er, C, aoffs, boffs, coffs, out_0,
         nc.scalar.copy(da[0][:, halves[1]], acc01[:])
         nc.scalar.copy(da[1][:, halves[0]], acc10[:])
         nc.scalar.copy(da[1][:, halves[1]], acc11[:])
-        nc.vector.tensor_copy(window[0][:].indirect(offsets(a_list, halves[0])), da[0][:, halves[0]])
-        quantise_core(2)
+        nc.vector.tensor_copy(window[0][:].indirect(a_list[:]), da[0][:])
         acc30 = product(3, halves[0])
         acc2 = product(2, whole)
         acc31 = product(3, halves[1])
-        nc.vector.tensor_copy(window[0][:].indirect(offsets(a_list, halves[1])), da[0][:, halves[1]])
         store(0)
         scalar_scatter(1, halves[0])
         nc.scalar.copy(da[3][:, halves[0]], acc30[:])

@@ -22,10 +22,9 @@ N = 512
 T = 2048
 U = 1024
 STORES = (768, 768, 512)
-GROUPS = (1536, 512)
-SCALAR_RUNS = (1, 3, 5, 7)
 RUN = 256
 VECTOR_ENTRIES = 128
+HIGH_DEAL = 32
 
 FLOPS = 2 * F * D * N
 
@@ -73,7 +72,7 @@ def tile_attend_gtucker_pl_kernel(tc, bT, cT, er, C, aoffs, boffs, coffs, out_0,
         make_identity(nc, identity[:])
         er_wide = sb.tile([P, LANES, P], F32, name="er_wide")
         nc.scalar.copy(er_wide[:], er_col[:].unsqueeze(2).to_broadcast([P, LANES, P]))
-        er_bank = psum.tile([P, LANES, P], F32, name="er_bank")
+        er_bank = psum.tile([P, LANES, P], F32, name="er_bank", tag="bank0")
         for m in range(LANES):
             nc.tensor.transpose(er_bank[:, m, :], er_wide[:, m, :], identity[:])
 
@@ -126,10 +125,10 @@ def tile_attend_gtucker_pl_kernel(tc, bT, cT, er, C, aoffs, boffs, coffs, out_0,
         def quantise_q(h):
             nc.vector.quantize_mx(out=q_codes[:, halves[h]].bitcast(E5M2), scales=q_scales[:, halves[h]], in_=q_bf[h][:].rearrange("p i t -> p (i t)"))
 
-        def deal_core(copy, g):
+        def deal_core(copy, g, first, last):
             copy(
-                core_bf[g][:].rearrange("p e m j -> p m j e"),
-                core[:].rearrange("p j (m t) -> p m j t", t=LANES)[:, :, :, 2 * g:2 * g + 2],
+                core_bf[g][:, :, first:last, :].rearrange("p e m j -> p m j e"),
+                core[:].rearrange("p j (m t) -> p m j t", t=LANES)[:, first:last, :, 2 * g:2 * g + 2],
             )
 
         def quantise_core(g, first, last):
@@ -141,16 +140,17 @@ def tile_attend_gtucker_pl_kernel(tc, bT, cT, er, C, aoffs, boffs, coffs, out_0,
 
         round_q(nc.vector.tensor_copy, 0)
         round_q(nc.scalar.copy, 1)
-        deal_core(nc.vector.tensor_copy, 0)
+        deal_core(nc.vector.tensor_copy, 0, 0, P)
         quantise_q(0)
         quantise_core(0, 0, 1)
         quantise_q(1)
         quantise_core(0, 1, 2)
-        deal_core(nc.scalar.copy, 1)
+        deal_core(nc.scalar.copy, 1, HIGH_DEAL, P)
+        deal_core(nc.vector.tensor_copy, 1, 0, HIGH_DEAL)
         quantise_core(1, 0, 2)
 
-        def product(t, run):
-            acc = psum.tile([P, run.stop - run.start], F32, name="acc%d_%d" % (t, run.start))
+        def product(t, run, bank):
+            acc = psum.tile([P, run.stop - run.start], F32, name="acc%d_%d" % (t, run.start), tag="bank%d" % bank)
             nc.tensor.matmul_mx(
                 out=acc[:],
                 lhsT=core_codes[t // 2][:, t % 2, :].bitcast(E4M3),
@@ -162,14 +162,14 @@ def tile_attend_gtucker_pl_kernel(tc, bT, cT, er, C, aoffs, boffs, coffs, out_0,
             )
             return acc
 
-        acc00 = product(0, halves[0])
-        acc01 = product(0, halves[1])
-        acc10 = product(1, halves[0])
-        acc11 = product(1, halves[1])
+        acc00 = product(0, halves[0], 1)
+        acc01 = product(0, halves[1], 2)
+        acc1 = product(1, whole, 3)
 
         da = [sb.tile([P, N], F32, name="da%d" % t) for t in range(LANES)]
-        groups = [slice(sum(GROUPS[:k]), sum(GROUPS[:k + 1])) for k in range(len(GROUPS))]
-        planar = [sb.tile([P, LANES, w], BF16, name="planar%d" % k, align_bytes=64) for k, w in enumerate(GROUPS)]
+        woven = list(range(T // RUN // 2))
+        turned = list(range(T // RUN // 2, T // RUN))
+        planar = sb.tile([P, LANES, len(woven) * RUN], BF16, name="planar", align_bytes=64)
         y_bf = [sb.tile([P, RUN, LANES], BF16, name="y_bf%d" % u, align_bytes=64) for u in range(T // RUN)]
         y_scales = sb.tile([P, T // LANES], U8, name="y_scales", align_bytes=64)
         y_codes = [sb.tile([P, w], U32, name="y_codes%d" % s, align_bytes=64) for s, w in enumerate(STORES)]
@@ -181,22 +181,19 @@ def tile_attend_gtucker_pl_kernel(tc, bT, cT, er, C, aoffs, boffs, coffs, out_0,
         def store(t):
             nc.sync.dma_start(out_rows[:, t, :], window[t][:])
 
-        def round_lane(copy, t, k):
-            copy(planar[k][:, t, :], window[t][:, groups[k]])
+        def round_lane(copy, t):
+            copy(planar[:, t, :], window[t][:, 0:len(woven) * RUN])
 
         nc.scalar.copy(da[0][:, halves[0]], acc00[:])
         nc.scalar.copy(da[0][:, halves[1]], acc01[:])
-        nc.scalar.copy(da[1][:, halves[0]], acc10[:])
-        nc.scalar.copy(da[1][:, halves[1]], acc11[:])
+        nc.scalar.copy(da[1][:], acc1[:])
         nc.vector.tensor_copy(window[0][:].indirect(a_list[:]), da[0][:])
-        acc30 = product(3, halves[0])
-        acc2 = product(2, whole)
-        acc31 = product(3, halves[1])
+        acc3 = product(3, whole, 4)
+        acc2 = product(2, whole, 5)
         store(0)
         scalar_scatter(1, halves[0])
-        nc.scalar.copy(da[3][:, halves[0]], acc30[:])
+        nc.scalar.copy(da[3][:], acc3[:])
         nc.scalar.copy(da[2][:], acc2[:])
-        nc.scalar.copy(da[3][:, halves[1]], acc31[:])
         nc.vector.tensor_copy(window[3][:].indirect(offsets(a_list, halves[0])), da[3][:, halves[0]])
         scalar_scatter(1, halves[1])
         store(1)
@@ -205,30 +202,61 @@ def tile_attend_gtucker_pl_kernel(tc, bT, cT, er, C, aoffs, boffs, coffs, out_0,
         nc.vector.tensor_copy(window[2][:].indirect(a_list[:]), da[2][:])
         store(2)
 
-        last = len(GROUPS) - 1
-        for k in range(len(GROUPS)):
-            round_lane(nc.gpsimd.tensor_copy, 0, k)
-        for k in range(last):
-            round_lane(nc.gpsimd.tensor_copy, 1, k)
-        round_lane(nc.scalar.copy, 1, last)
-        for k in range(len(GROUPS)):
-            round_lane(nc.scalar.copy, 3, k)
-        for k in range(len(GROUPS)):
-            round_lane(nc.vector.tensor_copy, 2, k)
+        for t in (0, 1, 3):
+            round_lane(nc.gpsimd.tensor_copy, t)
+        round_lane(nc.vector.tensor_copy, 2)
 
-        def weave(copy, u, first, width):
-            k = [j for j in range(len(GROUPS)) if groups[j].start <= u * RUN][-1]
-            column = u * RUN - groups[k].start + first
-            copy(
-                y_bf[u][:, first:first + width, :].rearrange("p (c i) t -> p c t i", i=4),
-                planar[k][:, :, column:column + width].rearrange("p t (c i) -> p c t i", i=4),
+        blocks = RUN // P
+
+        def turn_lane(bank, u, t):
+            for b in range(blocks):
+                first = u * RUN + b * P
+                nc.tensor.transpose(bank[:, b, t % 2, :], window[t][:, first:first + P], identity[:])
+
+        def round_pair(bank, u, g):
+            pairs = sb.tile([P, blocks, P, 2], BF16, name="pairs%d_%d" % (u, g))
+            nc.scalar.copy(pairs[:], bank[:].rearrange("c b e p -> c b p e"))
+            return pairs
+
+        def turn_back(bank, pairs, g):
+            for b in range(blocks):
+                nc.tensor.transpose(bank[:, b, g, :], pairs[:, b, :, :].rearrange("c p e -> c (p e)").bitcast(F32), identity[:])
+
+        low = {u: psum.tile([P, blocks, 2, P], F32, name="low%d" % u, tag="bank%d" % k) for k, u in enumerate(turned)}
+        high = {u: psum.tile([P, blocks, 2, P], F32, name="high%d" % u, tag="bank%d" % (k + len(turned))) for k, u in enumerate(turned)}
+        for t in (0, 1):
+            for u in turned:
+                turn_lane(low[u], u, t)
+        for u in turned:
+            turn_lane(high[u], u, 3)
+        low_pairs = {u: round_pair(low[u], u, 0) for u in turned}
+        back = {u: psum.tile([P, blocks, 2, P], F32, name="back%d" % u, tag="bank%d" % k) for k, u in enumerate(turned)}
+        for u in turned:
+            turn_lane(high[u], u, 2)
+        for u in turned:
+            turn_back(back[u], low_pairs[u], 0)
+
+        def finish_turned(u):
+            nc.scalar.copy(
+                y_bf[u][:].rearrange("p c t -> p (c t)").bitcast(F32).rearrange("p (b c g) -> p b c g", b=blocks, g=2),
+                back[u][:].rearrange("p b g c -> p b c g"),
             )
 
+        def weave(u):
+            nc.vector.tensor_copy(
+                y_bf[u][:].rearrange("p (c i) t -> p c t i", i=4),
+                planar[:, :, u * RUN:(u + 1) * RUN].rearrange("p t (c i) -> p c t i", i=4),
+            )
+
+        for k, u in enumerate(turned):
+            turn_back(back[u], round_pair(high[u], u, 1), 1)
+            if k > 0:
+                finish_turned(turned[k - 1])
+        finish_turned(turned[-1])
+
         for u in range(T // RUN):
-            if u in SCALAR_RUNS:
-                weave(nc.scalar.copy, u, 0, RUN)
-            else:
-                weave(nc.vector.tensor_copy, u, 0, RUN)
+            if u in woven:
+                weave(u)
             start = u * RUN
             plane, byte = divmod(start, T // LANES)
             s = [j for j in range(len(STORES)) if stored[j].start <= start][-1]

@@ -24,7 +24,10 @@ U = 1024
 STORES = (768, 768, 512)
 RUN = 256
 VECTOR_ENTRIES = 128
-HIGH_DEAL = 32
+FUSED = 160
+MIDDLE = 352
+LOW_DEAL = 80
+HIGH_DEAL = 48
 
 FLOPS = 2 * F * D * N
 
@@ -83,16 +86,20 @@ def tile_attend_gtucker_pl_kernel(tc, bT, cT, er, C, aoffs, boffs, coffs, out_0,
         gb = [sb.tile([P, N], F32, name="gb%d" % t) for t in range(LANES)]
         eb = [sb.tile([P, N], F32, name="eb%d" % t) for t in range(LANES)]
         gc = [sb.tile([P, N], F32, name="gc%d" % t) for t in range(LANES)]
-        q = [shared.tile([P, LANES, hn], F32, name="q%d" % h, offset=h * LANES * hn * 4, align_bytes=64) for h in range(2)]
-        q_bf = [sb.tile([P, hn, LANES], BF16, name="q_bf%d" % h, align_bytes=64) for h in range(2)]
+        q_fused = sb.tile([P, LANES, FUSED], F32, name="q_fused")
+        rest_runs = [slice(FUSED, MIDDLE), slice(MIDDLE, N)]
+        q_rest = [shared.tile([P, LANES, run.stop - run.start], F32, name="q_rest%d" % k, offset=k * 4096, align_bytes=64) for k, run in enumerate(rest_runs)]
+        q_bf = sb.tile([P, N, LANES], BF16, name="q_bf", align_bytes=64)
         q_codes = sb.tile([P, N], U32, name="q_codes", align_bytes=64)
         q_scales = sb.tile([P, N], U8, name="q_scales", align_bytes=64)
-        core_bf = [shared.tile([P, 2, P, LANES], BF16, name="core_bf%d" % g, offset=g * 2 * P * LANES * 2, align_bytes=64) for g in range(2)]
+        core_bf = [shared.tile([P, 2, P, LANES], BF16, name="core_bf%d" % g, offset=g * 4096, align_bytes=64) for g in range(2)]
         core_codes = [sb.tile([P, 2, P], U32, name="core_codes%d" % g, align_bytes=64) for g in range(2)]
         core_scales = [sb.tile([P, 2, P], U8, name="core_scales%d" % g, align_bytes=64) for g in range(2)]
 
         def offsets(index, run):
             return index[:, run.start // 16:run.stop // 16]
+
+        fused = slice(0, FUSED)
 
         def split(first):
             return slice(0, first), slice(first, N)
@@ -108,22 +115,20 @@ def tile_attend_gtucker_pl_kernel(tc, bT, cT, er, C, aoffs, boffs, coffs, out_0,
                 MULT,
             )
         for t in range(LANES):
-            on_vector, on_scalar = split(hn if t == LANES - 1 else VECTOR_ENTRIES)
-            nc.scalar.activation(gc[t][:, on_scalar], c_tab[t][:].indirect(offsets(c_list, on_scalar)), COPY)
-            nc.vector.tensor_tensor(q[0][:, t, on_vector], c_tab[t][:].indirect(offsets(c_list, on_vector)), eb[t][:, on_vector], MULT)
-            if on_scalar.start < hn:
-                rest = slice(on_scalar.start, hn)
-                nc.vector.tensor_tensor(q[0][:, t, rest], gc[t][:, rest], eb[t][:, rest], MULT)
-            nc.vector.tensor_tensor(q[1][:, t, :], gc[t][:, halves[1]], eb[t][:, halves[1]], MULT)
+            for run in rest_runs:
+                nc.scalar.activation(gc[t][:, run], c_tab[t][:].indirect(offsets(c_list, run)), COPY)
+            nc.vector.tensor_tensor(q_fused[:, t, :], c_tab[t][:].indirect(offsets(c_list, fused)), eb[t][:, fused], MULT)
+            for k, run in enumerate(rest_runs):
+                nc.vector.tensor_tensor(q_rest[k][:, t, :], gc[t][:, run], eb[t][:, run], MULT)
 
-        def round_q(copy, h):
+        def round_q(copy, run, values):
             copy(
-                q_bf[h][:].rearrange("p (c i) t -> p c t i", i=4),
-                q[h][:].rearrange("p t (c i) -> p c t i", i=4),
+                q_bf[:, run, :].rearrange("p (c i) t -> p c t i", i=4),
+                values.rearrange("p t (c i) -> p c t i", i=4),
             )
 
         def quantise_q(h):
-            nc.vector.quantize_mx(out=q_codes[:, halves[h]].bitcast(E5M2), scales=q_scales[:, halves[h]], in_=q_bf[h][:].rearrange("p i t -> p (i t)"))
+            nc.vector.quantize_mx(out=q_codes[:, halves[h]].bitcast(E5M2), scales=q_scales[:, halves[h]], in_=q_bf[:, halves[h], :].rearrange("p i t -> p (i t)"))
 
         def deal_core(copy, g, first, last):
             copy(
@@ -138,15 +143,17 @@ def tile_attend_gtucker_pl_kernel(tc, bT, cT, er, C, aoffs, boffs, coffs, out_0,
                 in_=core_bf[g][:, first:last, :, :].rearrange("p e m j -> p (e m j)"),
             )
 
-        round_q(nc.vector.tensor_copy, 0)
-        round_q(nc.scalar.copy, 1)
-        deal_core(nc.vector.tensor_copy, 0, 0, P)
+        round_q(nc.scalar.copy, fused, q_fused[:])
+        for k, run in enumerate(rest_runs):
+            round_q(nc.vector.tensor_copy, run, q_rest[k][:])
+        deal_core(nc.scalar.copy, 0, LOW_DEAL, P)
+        deal_core(nc.vector.tensor_copy, 0, 0, LOW_DEAL)
         quantise_q(0)
         quantise_core(0, 0, 1)
         quantise_q(1)
-        quantise_core(0, 1, 2)
         deal_core(nc.scalar.copy, 1, HIGH_DEAL, P)
         deal_core(nc.vector.tensor_copy, 1, 0, HIGH_DEAL)
+        quantise_core(0, 1, 2)
         quantise_core(1, 0, 2)
 
         def product(t, run, bank):

@@ -23,9 +23,10 @@ T = 2048
 U = 1024
 STORES = (768, 768, 512)
 RUN = 256
-VECTOR_ENTRIES = 128
-FUSED = 160
-MIDDLE = 352
+VECTOR_ENTRIES = 192
+FUSED = 224
+MIDDLE = 384
+SCALAR_ROUNDS = 160
 LOW_DEAL = 80
 HIGH_DEAL = 48
 
@@ -85,10 +86,11 @@ def tile_attend_gtucker_pl_kernel(tc, bT, cT, er, C, aoffs, boffs, coffs, out_0,
 
         gb = [sb.tile([P, N], F32, name="gb%d" % t) for t in range(LANES)]
         eb = [sb.tile([P, N], F32, name="eb%d" % t) for t in range(LANES)]
-        gc = [sb.tile([P, N], F32, name="gc%d" % t) for t in range(LANES)]
-        q_fused = sb.tile([P, LANES, FUSED], F32, name="q_fused")
+        gc = [sb.tile([P, N], F32, name="gc%d" % t) for t in range(LANES - 1)]
+        gc.append(shared.tile([P, N], F32, name="gc3", offset=0, align_bytes=64))
         rest_runs = [slice(FUSED, MIDDLE), slice(MIDDLE, N)]
-        q_rest = [shared.tile([P, LANES, run.stop - run.start], F32, name="q_rest%d" % k, offset=k * 4096, align_bytes=64) for k, run in enumerate(rest_runs)]
+        q_front = sb.tile([P, LANES, MIDDLE], F32, name="q_front")
+        q_back = shared.tile([P, LANES, N - MIDDLE], F32, name="q_back", offset=4096, align_bytes=64)
         q_bf = sb.tile([P, N, LANES], BF16, name="q_bf", align_bytes=64)
         q_codes = sb.tile([P, N], U32, name="q_codes", align_bytes=64)
         q_scales = sb.tile([P, N], U8, name="q_scales", align_bytes=64)
@@ -117,9 +119,9 @@ def tile_attend_gtucker_pl_kernel(tc, bT, cT, er, C, aoffs, boffs, coffs, out_0,
         for t in range(LANES):
             for run in rest_runs:
                 nc.scalar.activation(gc[t][:, run], c_tab[t][:].indirect(offsets(c_list, run)), COPY)
-            nc.vector.tensor_tensor(q_fused[:, t, :], c_tab[t][:].indirect(offsets(c_list, fused)), eb[t][:, fused], MULT)
-            for k, run in enumerate(rest_runs):
-                nc.vector.tensor_tensor(q_rest[k][:, t, :], gc[t][:, run], eb[t][:, run], MULT)
+            nc.vector.tensor_tensor(q_front[:, t, fused], c_tab[t][:].indirect(offsets(c_list, fused)), eb[t][:, fused], MULT)
+            for run, values in zip(rest_runs, (q_front[:, t, rest_runs[0]], q_back[:, t, :])):
+                nc.vector.tensor_tensor(values, gc[t][:, run], eb[t][:, run], MULT)
 
         def round_q(copy, run, values):
             copy(
@@ -143,9 +145,9 @@ def tile_attend_gtucker_pl_kernel(tc, bT, cT, er, C, aoffs, boffs, coffs, out_0,
                 in_=core_bf[g][:, first:last, :, :].rearrange("p e m j -> p (e m j)"),
             )
 
-        round_q(nc.scalar.copy, fused, q_fused[:])
-        for k, run in enumerate(rest_runs):
-            round_q(nc.vector.tensor_copy, run, q_rest[k][:])
+        round_q(nc.scalar.copy, slice(0, SCALAR_ROUNDS), q_front[:, :, 0:SCALAR_ROUNDS])
+        round_q(nc.vector.tensor_copy, slice(SCALAR_ROUNDS, MIDDLE), q_front[:, :, SCALAR_ROUNDS:MIDDLE])
+        round_q(nc.vector.tensor_copy, rest_runs[1], q_back[:])
         deal_core(nc.scalar.copy, 0, LOW_DEAL, P)
         deal_core(nc.vector.tensor_copy, 0, 0, LOW_DEAL)
         quantise_q(0)

@@ -24,8 +24,8 @@ U = 1024
 STORES = (768, 768, 512)
 RUN = 256
 VECTOR_ENTRIES = 192
-FUSED = 224
-MIDDLE = 384
+FUSED = 192
+MIDDLE = 352
 SCALAR_ROUNDS = 160
 LOW_DEAL = 80
 HIGH_DEAL = 48
@@ -106,16 +106,20 @@ def tile_attend_gtucker_pl_kernel(tc, bT, cT, er, C, aoffs, boffs, coffs, out_0,
         def split(first):
             return slice(0, first), slice(first, N)
 
-        for t in range(LANES):
-            on_vector, on_scalar = split(VECTOR_ENTRIES)
+        def by_lane(values):
+            return values.rearrange("p (n m) -> p n m", m=LANES)
+
+        on_vector, on_scalar = split(VECTOR_ENTRIES)
+        er_spread = er_bank[:].rearrange("p m n -> p n m")
+        er_front = sb.tile([P, VECTOR_ENTRIES], F32, name="er_front")
+        nc.scalar.activation(gb[0][:, on_scalar], b_tab[0][:].indirect(offsets(b_list, on_scalar)), COPY)
+        nc.vector.tensor_copy(gb[0][:, on_vector], b_tab[0][:].indirect(offsets(b_list, on_vector)))
+        nc.vector.tensor_copy(by_lane(er_front[:]), er_spread[:, 0:VECTOR_ENTRIES // LANES, :])
+        nc.vector.tensor_tensor(by_lane(eb[0][:]), by_lane(gb[0][:]), er_spread, MULT)
+        for t in range(1, LANES):
             nc.scalar.activation(gb[t][:, on_scalar], b_tab[t][:].indirect(offsets(b_list, on_scalar)), COPY)
-            nc.vector.tensor_copy(gb[t][:, on_vector], b_tab[t][:].indirect(offsets(b_list, on_vector)))
-            nc.vector.tensor_tensor(
-                eb[t][:].rearrange("p (n m) -> p n m", m=LANES),
-                gb[t][:].rearrange("p (n m) -> p n m", m=LANES),
-                er_bank[:].rearrange("p m n -> p n m"),
-                MULT,
-            )
+            nc.vector.tensor_tensor(eb[t][:, on_vector], b_tab[t][:].indirect(offsets(b_list, on_vector)), er_front[:], MULT)
+            nc.vector.tensor_tensor(by_lane(eb[t][:, on_scalar]), by_lane(gb[t][:, on_scalar]), er_spread[:, VECTOR_ENTRIES // LANES:, :], MULT)
         for t in range(LANES):
             for run in rest_runs:
                 nc.scalar.activation(gc[t][:, run], c_tab[t][:].indirect(offsets(c_list, run)), COPY)

@@ -23,6 +23,7 @@ T = 2048
 U = 1024
 STORES = (768, 768, 512)
 RUN = 256
+GROUPS = 2
 VECTOR_ENTRIES = 192
 FUSED = 192
 MIDDLE = 352
@@ -182,7 +183,8 @@ def tile_attend_gtucker_pl_kernel(tc, bT, cT, er, C, aoffs, boffs, coffs, out_0,
         da = [sb.tile([P, N], F32, name="da%d" % t) for t in range(LANES)]
         woven = list(range(T // RUN // 2))
         turned = list(range(T // RUN // 2, T // RUN))
-        planar = sb.tile([P, LANES, len(woven) * RUN], BF16, name="planar", align_bytes=64)
+        group = len(woven) * RUN // GROUPS
+        planar = sb.tile([P, GROUPS, LANES, group], BF16, name="planar", align_bytes=64)
         y_bf = [sb.tile([P, RUN, LANES], BF16, name="y_bf%d" % u, align_bytes=64) for u in range(T // RUN)]
         y_scales = sb.tile([P, T // LANES], U8, name="y_scales", align_bytes=64)
         y_codes = [sb.tile([P, w], U32, name="y_codes%d" % s, align_bytes=64) for s, w in enumerate(STORES)]
@@ -194,8 +196,8 @@ def tile_attend_gtucker_pl_kernel(tc, bT, cT, er, C, aoffs, boffs, coffs, out_0,
         def store(t):
             nc.sync.dma_start(out_rows[:, t, :], window[t][:])
 
-        def round_lane(copy, t):
-            copy(planar[:, t, :], window[t][:, 0:len(woven) * RUN])
+        def round_lane(copy, t, first, last):
+            copy(planar[:, first:last, t, :], window[t][:, first * group:last * group].rearrange("p (k c) -> p k c", c=group))
 
         nc.scalar.copy(da[0][:, halves[0]], acc00[:])
         nc.scalar.copy(da[0][:, halves[1]], acc01[:])
@@ -216,8 +218,9 @@ def tile_attend_gtucker_pl_kernel(tc, bT, cT, er, C, aoffs, boffs, coffs, out_0,
         store(2)
 
         for t in (0, 1, 3):
-            round_lane(nc.gpsimd.tensor_copy, t)
-        round_lane(nc.vector.tensor_copy, 2)
+            round_lane(nc.gpsimd.tensor_copy, t, 0, GROUPS)
+        for k in range(GROUPS):
+            round_lane(nc.vector.tensor_copy, 2, k, k + 1)
 
         blocks = RUN // P
 
@@ -256,9 +259,10 @@ def tile_attend_gtucker_pl_kernel(tc, bT, cT, er, C, aoffs, boffs, coffs, out_0,
             )
 
         def weave(u):
+            k, first = divmod(u * RUN, group)
             nc.vector.tensor_copy(
                 y_bf[u][:].rearrange("p (c i) t -> p c t i", i=4),
-                planar[:, :, u * RUN:(u + 1) * RUN].rearrange("p t (c i) -> p c t i", i=4),
+                planar[:, k, :, first:first + RUN].rearrange("p t (c i) -> p c t i", i=4),
             )
 
         for k, u in enumerate(turned):

@@ -29,7 +29,7 @@ FUSED = 192
 MIDDLE = 352
 SCALAR_ROUNDS = 160
 LOW_DEAL = 80
-HIGH_DEAL = 48
+HIGH_DEAL = 32
 
 FLOPS = 2 * F * D * N
 
@@ -134,8 +134,8 @@ def tile_attend_gtucker_pl_kernel(tc, bT, cT, er, C, aoffs, boffs, coffs, out_0,
                 values.rearrange("p t (c i) -> p c t i", i=4),
             )
 
-        def quantise_q(h):
-            nc.vector.quantize_mx(out=q_codes[:, halves[h]].bitcast(E5M2), scales=q_scales[:, halves[h]], in_=q_bf[:, halves[h], :].rearrange("p i t -> p (i t)"))
+        def quantise_q(run):
+            nc.vector.quantize_mx(out=q_codes[:, run].bitcast(E5M2), scales=q_scales[:, run], in_=q_bf[:, run, :].rearrange("p i t -> p (i t)"))
 
         def deal_core(copy, g, first, last):
             copy(
@@ -155,9 +155,11 @@ def tile_attend_gtucker_pl_kernel(tc, bT, cT, er, C, aoffs, boffs, coffs, out_0,
         round_q(nc.vector.tensor_copy, rest_runs[1], q_back[:])
         deal_core(nc.scalar.copy, 0, LOW_DEAL, P)
         deal_core(nc.vector.tensor_copy, 0, 0, LOW_DEAL)
-        quantise_q(0)
+        quarters = [slice(hn, hn + P), slice(hn + P, N)]
+        quantise_q(halves[0])
         quantise_core(0, 0, 1)
-        quantise_q(1)
+        for run in quarters:
+            quantise_q(run)
         deal_core(nc.scalar.copy, 1, HIGH_DEAL, P)
         deal_core(nc.vector.tensor_copy, 1, 0, HIGH_DEAL)
         quantise_core(0, 1, 2)
@@ -177,7 +179,7 @@ def tile_attend_gtucker_pl_kernel(tc, bT, cT, er, C, aoffs, boffs, coffs, out_0,
             return acc
 
         acc00 = product(0, halves[0], 1)
-        acc01 = product(0, halves[1], 2)
+        acc01 = [product(0, run, bank) for run, bank in zip(quarters, (2, 6))]
         acc1 = product(1, whole, 3)
 
         da = [sb.tile([P, N], F32, name="da%d" % t) for t in range(LANES)]
@@ -199,8 +201,9 @@ def tile_attend_gtucker_pl_kernel(tc, bT, cT, er, C, aoffs, boffs, coffs, out_0,
         def round_lane(copy, t, first, last):
             copy(planar[:, first:last, t, :], window[t][:, first * group:last * group].rearrange("p (k c) -> p k c", c=group))
 
-        nc.scalar.copy(da[0][:, halves[0]], acc00[:])
-        nc.scalar.copy(da[0][:, halves[1]], acc01[:])
+        nc.vector.tensor_copy(da[0][:, halves[0]], acc00[:])
+        for run, acc in zip(quarters, acc01):
+            nc.scalar.copy(da[0][:, run], acc[:])
         nc.scalar.copy(da[1][:], acc1[:])
         nc.vector.tensor_copy(window[0][:].indirect(a_list[:]), da[0][:])
         acc3 = product(3, whole, 4)

from contextlib import ExitStack

import concourse.mybir as mybir
from concourse.masks import make_identity

F32 = mybir.dt.float32
BF16 = mybir.dt.bfloat16
I32 = mybir.dt.int32
U32 = mybir.dt.uint32
U16 = mybir.dt.uint16
U8 = mybir.dt.uint8
E4M3 = mybir.dt.float8_e4m3fn_x4
E5M2 = mybir.dt.float8_e5m2_x4
MULT = mybir.AluOpType.mult
COPY = mybir.ActivationFunctionType.Copy

P = 128
LANES = 4
F = 512
D = 512
N = 512
T = 2048
U = 1024
STORES = (768, 768, 512)
RUN = 256
GROUPS = 2
VECTOR_ENTRIES = 192
FUSED = 192
MIDDLE = 352
SCALAR_ROUNDS = 160
LOW_DEAL = 80
HIGH_DEAL = 32

FLOPS = 2 * F * D * N


def tile_attend_gtucker_pl_kernel(tc, bT, cT, er, C, aoffs, boffs, coffs, out_0, out_1, out_2):
    nc = tc.nc
    with ExitStack() as ctx:
        lists = ctx.enter_context(tc.tile_pool(name="lists", bufs=1))
        sb = ctx.enter_context(tc.tile_pool(name="sb", bufs=1))
        shared = ctx.enter_context(tc.tile_pool(name="shared", bufs=1))
        psum = ctx.enter_context(tc.psum_pool(name="psum", bufs=1))

        a_list = lists.tile([P, N // 16], U16, name="a_list")
        b_list = lists.tile([P, N // 16], U16, name="b_list")
        c_list = lists.tile([P, N // 16], U16, name="c_list")

        b_rows = bT.rearrange("(p t) u -> p t u", t=LANES)
        c_rows = cT.rearrange("(p t) u -> p t u", t=LANES)
        core_rows = C.rearrange("(p j) d -> p j d", j=LANES)
        out_rows = out_0.rearrange("(p t) c -> p t c", t=LANES)
        out_words = out_1[0].rearrange("p c l -> p (c l)").bitcast(I32)
        out_scales = out_2[0].bitcast(I32)

        hn = N // 2
        halves = [slice(0, hn), slice(hn, N)]
        whole = slice(0, N)

        b_tab = [sb.tile([P, U], F32, name="b_tab%d" % t) for t in range(LANES)]
        c_tab = [sb.tile([P, U], F32, name="c_tab%d" % t) for t in range(LANES)]
        er_col = sb.tile([P, LANES], F32, name="er_col")
        core = sb.tile([P, LANES, D], F32, name="core")

        nc.sync.dma_start(er_col[:], er[0].rearrange("(p m) -> p m", m=LANES))
        nc.sync.dma_start(b_tab[0][:], b_rows[:, 0, :])
        nc.sync.dma_start(b_list[:], boffs)
        for t in range(1, LANES):
            nc.sync.dma_start(b_tab[t][:], b_rows[:, t, :])
        nc.sync.dma_start(c_list[:], coffs)
        for t in range(LANES):
            nc.sync.dma_start(c_tab[t][:], c_rows[:, t, :])
        nc.sync.dma_start(core[:], core_rows)
        nc.sync.dma_start(a_list[:], aoffs)

        identity = sb.tile([P, P], F32, name="identity")
        make_identity(nc, identity[:])
        er_wide = sb.tile([P, LANES, P], F32, name="er_wide")
        nc.scalar.copy(er_wide[:], er_col[:].unsqueeze(2).to_broadcast([P, LANES, P]))
        er_bank = psum.tile([P, LANES, P], F32, name="er_bank", tag="bank0")
        for m in range(LANES):
            nc.tensor.transpose(er_bank[:, m, :], er_wide[:, m, :], identity[:])

        window = [sb.tile([P, T], F32, name="window%d" % t) for t in range(LANES)]
        for t in range(LANES):
            nc.gpsimd.memset(window[t][:].bitcast(I32), 0)

        gb = [sb.tile([P, N], F32, name="gb%d" % t) for t in range(LANES)]
        eb = [sb.tile([P, N], F32, name="eb%d" % t) for t in range(LANES)]
        gc = [sb.tile([P, N], F32, name="gc%d" % t) for t in range(LANES - 1)]
        gc.append(shared.tile([P, N], F32, name="gc3", offset=0, align_bytes=64))
        rest_runs = [slice(FUSED, MIDDLE), slice(MIDDLE, N)]
        q_front = sb.tile([P, LANES, MIDDLE], F32, name="q_front")
        q_back = shared.tile([P, LANES, N - MIDDLE], F32, name="q_back", offset=4096, align_bytes=64)
        q_bf = sb.tile([P, N, LANES], BF16, name="q_bf", align_bytes=64)
        q_codes = sb.tile([P, N], U32, name="q_codes", align_bytes=64)
        q_scales = sb.tile([P, N], U8, name="q_scales", align_bytes=64)
        core_bf = [shared.tile([P, 2, P, LANES], BF16, name="core_bf%d" % g, offset=g * 4096, align_bytes=64) for g in range(2)]
        core_codes = [sb.tile([P, 2, P], U32, name="core_codes%d" % g, align_bytes=64) for g in range(2)]
        core_scales = [sb.tile([P, 2, P], U8, name="core_scales%d" % g, align_bytes=64) for g in range(2)]

        def offsets(index, run):
            return index[:, run.start // 16:run.stop // 16]

        fused = slice(0, FUSED)

        def split(first):
            return slice(0, first), slice(first, N)

        def by_lane(values):
            return values.rearrange("p (n m) -> p n m", m=LANES)

        on_vector, on_scalar = split(VECTOR_ENTRIES)
        er_spread = er_bank[:].rearrange("p m n -> p n m")
        er_front = sb.tile([P, VECTOR_ENTRIES], F32, name="er_front")
        nc.scalar.activation(gb[0][:, on_scalar], b_tab[0][:].indirect(offsets(b_list, on_scalar)), COPY)
        nc.vector.tensor_copy(gb[0][:, on_vector], b_tab[0][:].indirect(offsets(b_list, on_vector)))
        nc.vector.tensor_copy(by_lane(er_front[:]), er_spread[:, 0:VECTOR_ENTRIES // LANES, :])
        nc.vector.tensor_tensor(by_lane(eb[0][:]), by_lane(gb[0][:]), er_spread, MULT)
        for t in range(1, LANES):
            nc.scalar.activation(gb[t][:, on_scalar], b_tab[t][:].indirect(offsets(b_list, on_scalar)), COPY)
            nc.vector.tensor_tensor(eb[t][:, on_vector], b_tab[t][:].indirect(offsets(b_list, on_vector)), er_front[:], MULT)
            nc.vector.tensor_tensor(by_lane(eb[t][:, on_scalar]), by_lane(gb[t][:, on_scalar]), er_spread[:, VECTOR_ENTRIES // LANES:, :], MULT)
        for t in range(LANES):
            for run in rest_runs:
                nc.scalar.activation(gc[t][:, run], c_tab[t][:].indirect(offsets(c_list, run)), COPY)
            nc.vector.tensor_tensor(q_front[:, t, fused], c_tab[t][:].indirect(offsets(c_list, fused)), eb[t][:, fused], MULT)
            for run, values in zip(rest_runs, (q_front[:, t, rest_runs[0]], q_back[:, t, :])):
                nc.vector.tensor_tensor(values, gc[t][:, run], eb[t][:, run], MULT)

        def round_q(copy, run, values):
            copy(
                q_bf[:, run, :].rearrange("p (c i) t -> p c t i", i=4),
                values.rearrange("p t (c i) -> p c t i", i=4),
            )

        def quantise_q(run):
            nc.vector.quantize_mx(out=q_codes[:, run].bitcast(E5M2), scales=q_scales[:, run], in_=q_bf[:, run, :].rearrange("p i t -> p (i t)"))

        def deal_core(copy, g, first, last):
            copy(
                core_bf[g][:, :, first:last, :].rearrange("p e m j -> p m j e"),
                core[:].rearrange("p j (m t) -> p m j t", t=LANES)[:, first:last, :, 2 * g:2 * g + 2],
            )

        def quantise_core(g, first, last):
            nc.vector.quantize_mx(
                out=core_codes[g][:, first:last, :].rearrange("p e m -> p (e m)").bitcast(E4M3),
                scales=core_scales[g][:, first:last, :].rearrange("p e m -> p (e m)"),
                in_=core_bf[g][:, first:last, :, :].rearrange("p e m j -> p (e m j)"),
            )

        round_q(nc.scalar.copy, slice(0, SCALAR_ROUNDS), q_front[:, :, 0:SCALAR_ROUNDS])
        round_q(nc.vector.tensor_copy, slice(SCALAR_ROUNDS, MIDDLE), q_front[:, :, SCALAR_ROUNDS:MIDDLE])
        round_q(nc.vector.tensor_copy, rest_runs[1], q_back[:])
        deal_core(nc.scalar.copy, 0, LOW_DEAL, P)
        deal_core(nc.vector.tensor_copy, 0, 0, LOW_DEAL)
        quarters = [slice(hn, hn + P), slice(hn + P, N)]
        quantise_q(halves[0])
        quantise_core(0, 0, 1)
        for run in quarters:
            quantise_q(run)
        deal_core(nc.scalar.copy, 1, HIGH_DEAL, P)
        deal_core(nc.vector.tensor_copy, 1, 0, HIGH_DEAL)
        quantise_core(0, 1, 2)
        quantise_core(1, 0, 2)

        def product(t, run, bank):
            acc = psum.tile([P, run.stop - run.start], F32, name="acc%d_%d" % (t, run.start), tag="bank%d" % bank)
            nc.tensor.matmul_mx(
                out=acc[:],
                lhsT=core_codes[t // 2][:, t % 2, :].bitcast(E4M3),
                lhsT_scale=core_scales[t // 2][:, t % 2, :],
                rhs=q_codes[:, run].bitcast(E5M2),
                rhs_scale=q_scales[:, run],
                start=True,
                stop=True,
            )
            return acc

        acc00 = product(0, halves[0], 1)
        acc01 = [product(0, run, bank) for run, bank in zip(quarters, (2, 6))]
        acc1 = product(1, whole, 3)

        da = [sb.tile([P, N], F32, name="da%d" % t) for t in range(LANES)]
        woven = list(range(T // RUN // 2))
        turned = list(range(T // RUN // 2, T // RUN))
        group = len(woven) * RUN // GROUPS
        planar = sb.tile([P, GROUPS, LANES, group], BF16, name="planar", align_bytes=64)
        y_bf = [sb.tile([P, RUN, LANES], BF16, name="y_bf%d" % u, align_bytes=64) for u in range(T // RUN)]
        y_scales = sb.tile([P, T // LANES], U8, name="y_scales", align_bytes=64)
        y_codes = [sb.tile([P, w], U32, name="y_codes%d" % s, align_bytes=64) for s, w in enumerate(STORES)]
        stored = [slice(sum(STORES[:s]), sum(STORES[:s + 1])) for s in range(len(STORES))]

        def scalar_scatter(t, run):
            nc.scalar.activation(window[t][:].indirect(a_list[:, run.start // 16:run.stop // 16]), da[t][:, run], COPY)

        def store(t):
            nc.sync.dma_start(out_rows[:, t, :], window[t][:])

        def round_lane(copy, t, first, last):
            copy(planar[:, first:last, t, :], window[t][:, first * group:last * group].rearrange("p (k c) -> p k c", c=group))

        nc.vector.tensor_copy(da[0][:, halves[0]], acc00[:])
        for run, acc in zip(quarters, acc01):
            nc.scalar.copy(da[0][:, run], acc[:])
        nc.scalar.copy(da[1][:], acc1[:])
        nc.vector.tensor_copy(window[0][:].indirect(a_list[:]), da[0][:])
        acc3 = product(3, whole, 4)
        acc2 = product(2, whole, 5)
        store(0)
        scalar_scatter(1, halves[0])
        nc.scalar.copy(da[3][:], acc3[:])
        nc.scalar.copy(da[2][:], acc2[:])
        nc.vector.tensor_copy(window[3][:].indirect(offsets(a_list, halves[0])), da[3][:, halves[0]])
        scalar_scatter(1, halves[1])
        store(1)
        scalar_scatter(3, halves[1])
        store(3)
        nc.vector.tensor_copy(window[2][:].indirect(a_list[:]), da[2][:])
        store(2)

        for t in (0, 1, 3):
            round_lane(nc.gpsimd.tensor_copy, t, 0, GROUPS)
        for k in range(GROUPS):
            round_lane(nc.vector.tensor_copy, 2, k, k + 1)

        blocks = RUN // P

        def turn_lane(bank, u, t):
            for b in range(blocks):
                first = u * RUN + b * P
                nc.tensor.transpose(bank[:, b, t % 2, :], window[t][:, first:first + P], identity[:])

        def round_pair(bank, u, g):
            pairs = sb.tile([P, blocks, P, 2], BF16, name="pairs%d_%d" % (u, g))
            nc.scalar.copy(pairs[:], bank[:].rearrange("c b e p -> c b p e"))
            return pairs

        def turn_back(bank, pairs, g):
            for b in range(blocks):
                nc.tensor.transpose(bank[:, b, g, :], pairs[:, b, :, :].rearrange("c p e -> c (p e)").bitcast(F32), identity[:])

        low = {u: psum.tile([P, blocks, 2, P], F32, name="low%d" % u, tag="bank%d" % k) for k, u in enumerate(turned)}
        high = {u: psum.tile([P, blocks, 2, P], F32, name="high%d" % u, tag="bank%d" % (k + len(turned))) for k, u in enumerate(turned)}
        for t in (0, 1):
            for u in turned:
                turn_lane(low[u], u, t)
        for u in turned:
            turn_lane(high[u], u, 3)
        low_pairs = {u: round_pair(low[u], u, 0) for u in turned}
        back = {u: psum.tile([P, blocks, 2, P], F32, name="back%d" % u, tag="bank%d" % k) for k, u in enumerate(turned)}
        for u in turned:
            turn_lane(high[u], u, 2)
        for u in turned:
            turn_back(back[u], low_pairs[u], 0)

        def finish_turned(u):
            nc.scalar.copy(
                y_bf[u][:].rearrange("p c t -> p (c t)").bitcast(F32).rearrange("p (b c g) -> p b c g", b=blocks, g=2),
                back[u][:].rearrange("p b g c -> p b c g"),
            )

        def weave(u):
            k, first = divmod(u * RUN, group)
            nc.vector.tensor_copy(
                y_bf[u][:].rearrange("p (c i) t -> p c t i", i=4),
                planar[:, k, :, first:first + RUN].rearrange("p t (c i) -> p c t i", i=4),
            )

        for k, u in enumerate(turned):
            turn_back(back[u], round_pair(high[u], u, 1), 1)
            if k > 0:
                finish_turned(turned[k - 1])
        finish_turned(turned[-1])

        for u in range(T // RUN):
            if u in woven:
                weave(u)
            start = u * RUN
            plane, byte = divmod(start, T // LANES)
            s = [j for j in range(len(STORES)) if stored[j].start <= start][-1]
            word = start - stored[s].start
            nc.vector.quantize_mx(
                out=y_codes[s][:, word:word + RUN].bitcast(E4M3),
                scales=y_scales[LANES * plane:P, byte:byte + RUN],
                in_=y_bf[u][:].rearrange("p c t -> p (c t)"),
            )
            if start + RUN == stored[s].stop:
                nc.sync.dma_start(out_words[:, stored[s]], y_codes[s][:].bitcast(I32))
        for quad in range(4):
            queue = nc.scalar if quad % 2 == 0 else nc.sync
            queue.dma_start(out_scales[4 * quad:4 * quad + 4, :].rearrange("r (h x) -> h r x", h=LANES), y_scales[32 * quad:32 * quad + 16, :].bitcast(I32))
